import numpy as np, ml_dtypes
CORES = [16,18,20,22]
N = 4
BF = ml_dtypes.bfloat16
def gentries(a):
    return np.ascontiguousarray(a.reshape(8, 16, -1).transpose(0, 2, 1)).reshape(8, -1)
def gtable(e):
    e = np.asarray(e); return np.ascontiguousarray(e.reshape(8, -1, 16).transpose(0, 2, 1)).reshape(128, -1).astype(np.int32)
B, H, D, O, CAP, RO = 4096, 2048, 2048, 2048, 512, 3
K2, K3, K5 = 37, 611, 1237
def parts(rng):
    wt = (rng.choice(np.array([12, 20, 40, 64]), (N, 8, 16, 1)) * rng.random((N, 8, 16, B))).astype(np.int64)
    kid = rng.integers(0, B // 16, (N, 8, 16, B)); noise = rng.integers(0, 64, (N, 8, 16, H))
    for q in range(N):
        for g in rng.permutation(8)[:2]: kid[q, g] = rng.integers(0, B // 16, 8)[rng.integers(0, 8, (16, B))]
    room = np.minimum(rng.integers(60, 256, (N, 8, 1, D)) + rng.integers(0, 41, (N, 8, 16, D)), 255)
    room = np.where(rng.random(room.shape) < 0.01, rng.integers(0, 60, room.shape), room)
    need = (rng.integers(10, 201, (N, 8, 1, O)) * rng.random((N, 8, 16, O))).astype(np.int64)
    return wt, kid, noise, room, need, rng.integers(0, B, (N, 8, O)), rng.integers(0, H, (N, 8, O))
def sure(rng, wt, noise, q, g, win):
    noise[q, g] = rng.integers(8, 64, (16, H)); v = rng.integers(0, 8, (16, B)); v[win, np.arange(B)] = 63; wt[q, g] = v
def pack(wt, kid, noise, room, need, begin, salt):
    a = [np.ascontiguousarray(v.reshape(N, 128, -1)).astype(np.float32).astype(BF) for v in (wt, kid, noise, room, need)]
    return {"wt": a[0], "kid": a[1], "noise": a[2], "room": a[3], "need": a[4], "begin": np.stack([gtable(v) for v in begin]), "salt": np.stack([gtable(v) for v in salt])}
def setup_inputs(rng):
    return pack(*parts(rng))
def setup_inputs_cap(rng):
    wt, kid, noise, room, need, begin, salt = parts(rng)
    win = rng.integers(0, 16, (N, 8, B)); win[..., :16] = np.arange(16)
    win[:, 6] = (np.arange(B) & (N - 1)) + N * rng.integers(0, 16 // N, (N, B)); room[:, 6] = np.maximum(room[:, 6], 200)
    noise = rng.integers(8, 64, noise.shape); wt = rng.integers(0, 8, wt.shape); np.put_along_axis(wt, win[:, :, None, :], 63, 2)
    for q in range(N):
        for g in range(8):
            r = (q + 1 + int(rng.integers(0, N - 1))) % N; n = (CAP, CAP + 1, CAP - 1, 0, O, 1, CAP, CAP)[g]
            others = np.array([i for i in range(N) if i != r])
            to = rng.permutation(np.concatenate([np.full(n, r), rng.choice(others, O - n)]))
            if g < 2:
                i = np.flatnonzero(to == r)[-1]; to[i] = to[O - 1]; to[O - 1] = r
            if g == 6: to = rng.permutation(np.arange(O) & (N - 1))
            if g == 7:
                to = rng.choice(others, O); to[np.argsort(rng.permutation(16)[np.arange(O) % 16], kind="stable")[:n]] = r
            for i in range(N):
                m = np.flatnonzero(to == i); begin[q, g, m] = rng.choice(np.flatnonzero((win[q, g] & (N - 1)) == i), len(m))
    return pack(wt, kid, noise, room, need, begin, salt)
def setup_inputs_ties(rng):
    wt, kid, noise, room, need, begin, salt = parts(rng)
    wt = rng.integers(0, 3, wt.shape) * (rng.random((N, 8, 1, B)) > 0.1); noise = rng.integers(0, 3, noise.shape)
    wt = np.where(rng.random((N, 8, 1, B)) < 0.15, rng.integers(1, 3, (N, 8, 1, B)), wt)
    noise = np.where(rng.random((N, 8, 1, H)) < 0.15, rng.integers(1, 3, (N, 8, 1, H)), noise) * (rng.random((N, 8, 1, H)) > 0.05)
    room = np.where(rng.random(room.shape) < 0.003, 0, np.zeros(room.shape, np.int64) + rng.choice(np.array([99, 100, 100, 101, 255]), (N, 8, 1, D)))
    need = np.where(rng.random(need.shape) < 0.1, rng.choice(np.array([0, 99, 100, 101, 255]), (N, 8, 1, O)), 0)
    begin[:, 1::4] = rng.choice(np.array([0, B - 1]), (N, 2, O)); salt[:, 2::4] = rng.choice(np.array([0, H - 1]), (N, 2, O))
    kid[:, 7] = rng.integers(0, B // 16, (N, 16, B)); win = rng.integers(0, 16, (N, B))
    for q in range(N): sure(rng, wt, noise, q, 7, win[q])
    to = 16 * np.take_along_axis(kid[:, 7], win[:, None, :], 1)[:, 0] + win
    few = rng.integers(0, B, (N, 24)); begin[:, 7] = np.take_along_axis(few, rng.integers(0, 24, (N, O)), 1)
    need[:, 7] = np.maximum(need[:, 7], 1); room[:, 7] = 0
    for s in range(2 * (RO - 1), -1, -2):
        b = np.take_along_axis(to, (few + K5 * s) & (B - 1), 1); own = b & (N - 1)
        room[own, 7, :, to[own, b] & (D - 1)] = 255 if s == 2 * (RO - 1) else 0
    return pack(wt, kid, noise, room, need, begin, salt)
def setup_inputs_again(rng):
    wt, kid, noise, room, need, begin, salt = parts(rng)
    for q in range(N):
        for g in range(8): kid[q, g] = rng.integers(0, B // 16, 2)[rng.integers(0, 2, (16, B))]
        kid[q, 3] = rng.integers(0, B // 16); wt[q, 3] = 0; wt[q, 3, rng.integers(0, 16)] = 63
    noise[:, 3] = np.maximum(noise[:, 3], 1); room = np.maximum(room, 200)
    begin[:, ::2] = rng.choice(np.array([0, 5, B // 2, B - 1]), (N, 4, O)); salt[:, ::2] = rng.choice(np.array([0, 1, H // 2, H - 1]), (N, 4, O))
    r = int(rng.integers(0, N)); c = r + N * int(rng.integers(0, 16 // N))
    win = (np.arange(B) & (N - 1)) + N * rng.integers(0, 16 // N, (N, B)); win[r, r::N] = c; kid[r, 5, c, r::N] = kid[r, 5, c, r]
    for q in range(N): sure(rng, wt, noise, q, 5, win[q])
    begin[:, 5] = r + N * rng.integers(0, B // N, (N, O))
    return pack(wt, kid, noise, room, need, begin, salt)
def setup_inputs_full(rng):
    wt, kid, noise, room, need, begin, salt = parts(rng); q = rng.permutation(N)
    need = np.where(rng.random((N, 8, 1, O)) < 0.05, 255, np.maximum(need, 1)); room[q[0]] = 0; need[q[1]] = 0; room[q[2]] = 255
    r, a = int(q[2]), int(q[3]); walk = (K5 * np.arange(B)) & (B - 1)
    for g in range(8):
        win = rng.choice(np.array([c for c in range(16) if c & (N - 1) != r]), B); win[walk[::8]] = r + N * rng.integers(0, 16 // N, B // 8)
        sure(rng, wt, noise, a, g, win)
        at = rng.integers(1, 4, O); at[rng.permutation(O)[:CAP // 2]] = 0
        begin[a, g] = walk[8 * rng.integers(0, B // 8, O) + at]
    return pack(wt, kid, noise, room, need, begin, salt)
def setup_inputs_spread(rng):
    wt, kid, noise, room, need, begin, salt = parts(rng); ex = np.array([0.3, 1.0, 3.0])
    wt = np.minimum((64 * rng.random(wt.shape) ** rng.choice(ex, (N, 8, 1, B))).astype(np.int64), 63)
    noise = np.minimum((64 * rng.random(noise.shape) ** rng.choice(ex, (N, 8, 1, H))).astype(np.int64), 63)
    kid = np.minimum((B // 16 * rng.random(kid.shape) ** 3).astype(np.int64), B // 16 - 1)
    room = np.minimum((256 * rng.random(room.shape) ** rng.choice(np.array([0.0, 0.02, 0.1, 1.0]), (N, 8, 1, D))).astype(np.int64), 255)
    need = np.minimum((np.exp2(8 * rng.random((N, 8, 1, O))) * rng.random(need.shape)).astype(np.int64), 255)
    begin = np.minimum((B * rng.random((N, 8, O)) ** 2).astype(np.int64), B - 1); salt = np.minimum((H * rng.random((N, 8, O)) ** 3).astype(np.int64), H - 1)
    return pack(wt, kid, noise, room, need, begin, salt)
def check_inputs(d):
    bad = []
    for k, hi in (("wt", 63), ("kid", B // 16 - 1), ("noise", 63), ("room", 255), ("need", 255), ("begin", B - 1), ("salt", H - 1)):
        v = np.asarray(d[k]).astype(np.float32)
        if not np.all((v >= 0) & (v <= hi)): bad.append("range of " + k)
        if not np.all(v == np.floor(v)): bad.append("whole numbers in " + k)
    return bad
def columns(a):
    return np.ascontiguousarray(a.astype(np.float32).astype(np.int32).reshape(N, 8, 16, -1).transpose(0, 1, 3, 2))
def choose(w, k, z, r, b, h):
    g = np.arange(8)[None, :, None]
    c = np.argmax(w[r, g, b] * z[r, g, h], axis=-1)
    return 16 * k[r, g, b, c].astype(np.int64) + c
def reference(wt, kid, noise, room, need, begin, salt):
    w, k, z, rm, nd = columns(wt), columns(kid), columns(noise), columns(room), columns(need)
    be = np.stack([gentries(a) for a in begin]).astype(np.int64); sa = np.stack([gentries(a) for a in salt]).astype(np.int64)
    home = np.arange(N)[:, None, None]; g = np.arange(8)[None, :, None]
    t = np.zeros((N, 8, O), np.int64); one = np.full((N, 8, O), -1, np.int64); two = np.full((N, 8, O), -1, np.int64)
    for rnd in range(RO):
        takes = two < 0
        b0 = (be + K5 * t) & (B - 1)
        b1 = choose(w, k, z, home, b0, (sa + K2 * b0 + K3 * t) & (H - 1))
        own = b1 & (N - 1); goes = np.zeros((N, 8, O), bool)
        for r in range(N):
            m = (takes & (own == r)).astype(np.int64)
            goes = goes | ((m == 1) & (np.add.accumulate(m, axis=2) - m < CAP))
        d = choose(w, k, z, own, b1, (sa + K2 * b1 + K3 * t) & (H - 1)) & (D - 1)
        fits = np.all(nd <= rm[own, g, d], axis=-1)
        dev = own * D + d; keep = goes & fits & (dev != one)
        two = np.where(keep & (one >= 0), dev, two); one = np.where(keep & (one < 0), dev, one)
        t = t + np.where(goes, np.where(keep, 1, 2), 0)
    return {"ya": np.stack([gtable(a) for a in one]).astype(np.float32), "yb": np.stack([gtable(a) for a in two]).astype(np.float32)}

@@ -1,0 +1,568 @@
+import numpy as np
+from concourse.bass import DstId, RemoteDMATransfer
+from concourse.mybir import AluOpType as ALU, ActivationFunctionType as AF
+
+NR, B, H, D, O, CAP, RO = 4, 4096, 2048, 2048, 2048, 512, 3
+NC = 2
+S = 16 // NC
+NSH = 16 // S
+CW = 128 // NC
+NO = O // NC
+SW = NO + 16
+QW = 144
+ROOM_ON = "VVVVVV"
+ROUTE = "PVPVPVPVPVPV"
+KBIAS = -(1985 * 4096 + 2047.5)
+M12, M11, M8 = 1.5 * 2.0 ** 35, 1.5 * 2.0 ** 34, 1.5 * 2.0 ** 31
+WTW = 9056
+DB = [256, 1, 64, -64, -1, 2 ** 17, -37, -4, 8, -2048, 8192, -8192, -4096]
+DH = [4096, 1, 1237, -1237, -724, 724, 611, 2011]
+DF = [1, 592, 16]
+
+BF, F16, F32, I32, U16 = "bfloat16", "float16", "float32", "int32", "uint16"
+SB = {
+    "WT": (WTW, BF), "KD": (WTW, BF), "N1": (5120, BF), "NR0": (H, BF), "RM0": (D, BF), "ND0": (O, BF), "ND1": (O, BF),
+    "W2": (B, BF), "K2": (B, BF), "N2": (NR * H, BF), "R2": (NR * D, BF), "XU": (2048, U16), "XH": (1024, F16),
+    "LU": (6144, U16), "LH": (3072, F16), "SN": (1024, BF), "X32": (2048, F32), "GA": (O, BF), "GK": (O, BF),
+    "GP": (O, F16), "GR": (O, BF), "VI": (O, BF), "SC": (NC * SW, F32), "QB": (NC * QW, F32),
+    "BEG": (128, I32), "SAL": (128, I32), "I1": (128, I32), "I2": (128, I32), "I3": (128, I32), "I4": (128, I32),
+    "F1": (128, F32), "BB": (128, F16), "BA": (128, F16), "BS": (128, F16),
+    "OB": (128, U16), "OH": (128, U16), "OB2": (128, U16), "OH2": (128, U16), "OR": (128, U16), "OQ": (8, U16),
+    "HH": (128, F32), "QC": (128, F32), "H2": (128, F32), "T2": (128, F32),
+    "CP": (128, BF), "UP": (128, BF), "CP2": (128, BF), "MK": (512, BF), "IK": (512, BF), "SG": (512, BF),
+    "RS": (512, BF), "DL": (512, BF), "GS": (128, BF), "TT": (256, BF), "KP": (384, BF), "EQ": (128, BF), "BO": (128, BF),
+    "DV": (128, F32), "KV": (256, F32), "S12": (128, F32), "B12": (128, F32), "A12": (128, F32), "U1": (128, F32),
+    "U2": (128, F32), "NN": (128, F32), "DA": (128, F32), "DBB": (128, F32), "YA": (128, F32), "YB": (128, F32),
+    "ONE": (144, F32), "EE": (NSH * CW, F32), "PI": (2, I32), "PJ": (2, I32), "PF": (2, F32),
+    "JF": (144, F32), "MF": (128, F32), "OF": (8, F32), "OG": (8, F32),
+    "SEL": (144, BF), "BLK": (128, BF), "UT0": (128, BF), "UT": (128, BF),
+    "MB": (128 * len(DB), BF), "MH": (128 * len(DH), F16), "MFF": (128 * len(DF), F32),
+}
+SCRATCH = {k: ("sbuf", [128, w], t) for k, (w, t) in SB.items()}
+for _i in range(8):
+    SCRATCH["PS%d" % _i] = ("psum", [128, 512], F32)
+SEMAPHORES = ["cV", "cA", "cP", "cG", "sent"] + ["dm%d" % i for i in range(24)] + ["ar%d" % i for i in range(12)]
+
+CY, PCY, GF = 0.83e-3 * 1.25, 0.42e-3 * 1.25, 1.56
+LAT_X, LAT_S, RATE = 0.12, 0.08, 220e3
+TUNE, SIGMA, SLACK = 1500, 1.0, 0.2
+SKEW, PRE, PRE2, NB = 4.0, 5.0, 0.0, 15
+
+
+def build(g, T, topo, rank):
+    ops = []
+    acc = {}
+    cur = [-1]
+
+    def v(name, a=0, b=None, step=1):
+        if b is None:
+            b = T[name].shape[1]
+        ap = T[name][:, a:b] if step == 1 else T[name][:, a:b:step]
+        return (ap, [(name, a, b)], len(range(a, b, step)), SB[name][1] if name in SB else F32)
+
+    def ind(win, off):
+        return (win[0].indirect(off[0]), win[1] + off[1], 16 * off[2], win[3], True)
+
+    def add(q, fn, dur, reads, writes, kind="c", extra=()):
+        i = len(ops)
+        deps = set(extra)
+        for (n, a, b) in reads:
+            for (j, a2, b2, w) in acc.get(n, []):
+                if w and a < b2 and a2 < b:
+                    deps.add(j)
+        for (n, a, b) in writes:
+            for (j, a2, b2, w) in acc.get(n, []):
+                if a < b2 and a2 < b:
+                    deps.add(j)
+        for (n, a, b) in writes:
+            acc[n] = [e for e in acc.get(n, []) if not (a <= e[1] and e[2] <= b)] + [(i, a, b, True)]
+        for (n, a, b) in reads:
+            acc.setdefault(n, []).append((i, a, b, False))
+        deps.discard(i)
+        banks = set(n for (n, a, b) in reads + writes if n.startswith("PS"))
+        ops.append({"q": q, "fn": fn, "dur": dur, "deps": deps, "kind": kind, "banks": banks, "c": cur[0]})
+        return i
+
+    def vcost(out, ins, tt=False):
+        n = out[2]
+        if len(ins[0]) == 5:
+            return 0.05 + n * GF * CY
+        f = 0.5 if (all(x[3] in (BF, F16, U16) for x in [out] + ins) and not tt) else 1.0
+        if tt and not any(x[1][0][0].startswith("PS") for x in ins):
+            f = 2.0
+        return max(64, n * f) * CY + 0.03
+
+    def ts(out, in0, s1, s2, op0, op1=None):
+        r = in0[1] + (s1[1] if isinstance(s1, tuple) else [])
+        a1 = s1[0] if isinstance(s1, tuple) else s1
+        if op1 is None:
+            fn = lambda: g.vector.tensor_scalar(out[0], in0[0], a1, None, op0)
+        else:
+            fn = lambda: g.vector.tensor_scalar(out[0], in0[0], a1, s2, op0, op1)
+        return add("V", fn, vcost(out, [in0]), r, out[1])
+
+    def tt(out, in0, in1, op):
+        return add("V", lambda: g.vector.tensor_tensor(out[0], in0[0], in1[0], op), vcost(out, [in0, in1], True),
+                   in0[1] + in1[1], out[1])
+
+    def cp(out, in0):
+        return add("V", lambda: g.vector.tensor_copy(out[0], in0[0]), vcost(out, [in0]), in0[1], out[1])
+
+    def ms(out, c):
+        return add("V", lambda: g.vector.memset(out[0], c), vcost(out, [out]), [], out[1])
+
+    def scan(out, d0, d1, op0, op1, init=None):
+        i0, r = (init[0], init[1]) if init else (0.0, [])
+        return add("V", lambda: g.vector.tensor_tensor_scan(out[0], d0[0], d1[0], i0, op0, op1),
+                   vcost(out, [d0, d1]), d0[1] + d1[1] + r, out[1])
+
+    def act(out, in0, bias=0.0, scale=1.0, func=AF.Identity):
+        d = 0.065 + out[2] * GF * CY if len(in0) == 5 else max(64, out[2]) * CY + 0.03
+        return add("A", lambda: g.scalar.activation(out[0], in0[0], func, bias=float(bias), scale=float(scale)), d, in0[1], out[1])
+
+    def mm(groups):
+        r, w, d = [], [], 0.03
+        for out, terms in groups:
+            w += out[1]
+            for l, x in terms:
+                r += l[1] + x[1]
+                d += max(min(64, l[2]), x[2]) * (4 if l[3] == F32 else 1) * PCY
+
+        def fn():
+            last = None
+            for out, terms in groups:
+                for k, (l, x) in enumerate(terms):
+                    last = g.tensor.matmul(out[0], l[0], x[0], k == 0, k == len(terms) - 1)
+            return last
+        return add("P", fn, d, r, w)
+
+    def iota(out, pat, base, mult):
+        kw = {} if out[3] == I32 else {"allow_small_or_imprecise_dtypes": True}
+        return add("G", lambda: g.iota(out[0], pat, base, mult, **kw), 0.13 + 2 * out[2] * CY, [], out[1])
+
+    def asel(out, in0, pat, op, base, mult):
+        return add("G", lambda: g.affine_select(out[0], in0[0], pat, op, 0.0, base, mult), 0.17 + 2 * out[2] * CY, in0[1], out[1])
+
+    nd = [0]
+
+    def dma(out, in_, nbytes, reads, writes, extra=()):
+        i = add("S", lambda: g.sync.dma_start(out, in_), nbytes / RATE, reads, writes, "d", extra)
+        ops[i]["sem"] = (T.sem["dm%d" % nd[0]], 16)
+        nd[0] += 1
+        return i
+
+    def db(c):
+        return v("MB", 128 * DB.index(c), 128 * DB.index(c) + 128)
+
+    def dh(c):
+        return v("MH", 128 * DH.index(c), 128 * DH.index(c) + 128)
+
+    def df(c):
+        return v("MFF", 128 * DF.index(c), 128 * DF.index(c) + 128)
+
+    def w5(name, a, n=512):
+        return v(name, a, a + n)
+
+    prev = []
+
+    def loads(lst, extra=()):
+        for name, src, a, b in lst:
+            i = dma(v(name, a, b)[0], src[:, a:b], 128 * (b - a) * (4 if b == 128 else 2), [], [(name, a, b)], extra)
+            ops[i]["after"] = prev[-1:]
+            prev.append(i)
+    loads([("NR0", T.noise, 1024, 2048), ("RM0", T.room, 0, 1024), ("BEG", T.begin, 0, 128), ("SAL", T.salt, 0, 128),
+           ("WT", T.wt, 0, B), ("NR0", T.noise, 0, 1024)])
+
+    ms(v("ONE"), 1.0)
+    asel(df(1), v("ONE", 0, 128), [[-1, 128]], ALU.is_equal, 0, 1)
+    for c in DB:
+        act(db(c), df(1), 0.0, c)
+    for c in DH:
+        ts(dh(c), db(1), float(c), None, ALU.mult)
+    for c in DF[1:]:
+        act(df(c), df(1), 0.0, c)
+    for k in range(NSH):
+        asel(v("EE", k * CW, (k + 1) * CW), v("ONE", 0, CW), [[-NSH, CW]], ALU.is_equal, -k, 1)
+    iota(v("PI", 0, 1), [[0, 1]], 0, 1)
+    ts(v("PJ", 0, 1), v("PI", 0, 1), 112, None, ALU.bitwise_and)
+    ts(v("PJ", 1, 2), v("PI", 0, 1), 15, None, ALU.bitwise_and)
+    cp(v("PF", 0, 1), v("PJ", 0, 1))
+    ts(v("PF", 1, 2), v("PJ", 1, 2), 128.0, None, ALU.mult)
+    iota(v("JF"), [[1, 144]], -15, 0)
+    iota(v("MF"), [[16, 8], [0, 16]], 0, 0)
+    iota(v("OF"), [[16, 8]], 15, 0)
+    ts(v("SEL"), v("JF"), v("PF", 0, 1), None, ALU.is_equal)
+    ts(v("BLK"), v("MF"), v("PF", 0, 1), None, ALU.is_equal)
+    ts(v("OG"), v("OF"), v("PF", 1, 2), float(NO), ALU.add, ALU.min)
+    cp(v("OQ"), v("OG"))
+    asel(v("UT0"), v("BLK"), [[-1, 128]], ALU.is_gt, 0, 1)
+    tt(v("UT"), db(-4096), v("UT0"), ALU.subtract)
+    ms(v("DL"), 256.0)
+    ms(v("DL", 0, 512, 16), -2.0 ** 24)
+    ms(v("RS"), 1.0)
+    ms(v("RS", 0, 3 * CW + 1, CW), 0.0)
+    ms(v("QB"), 0.0)
+    for c in range(NC):
+        ms(v("SC", c * SW + NO, (c + 1) * SW), -KBIAS)
+
+    cp(v("OB"), v("BEG"))
+    ts(v("F1"), v("BEG"), 37.0, None, ALU.mult)
+    tt(v("I1"), v("F1"), v("SAL"), ALU.add)
+    ts(v("I2"), v("I1"), H - 1, None, ALU.bitwise_and)
+    cp(v("OH"), v("I2"))
+    ts(v("BB"), v("BEG"), -2048.0, None, ALU.add)
+    ts(v("BA"), v("I2"), -1024.0, None, ALU.add)
+    ts(v("I3"), v("SAL"), 35.0, None, ALU.add)
+    ts(v("I4"), v("I3"), H - 1, None, ALU.bitwise_and)
+    ts(v("BS"), v("I4"), -1023.5, None, ALU.add)
+
+    xb = [0]
+
+    def xbank():
+        xb[0] += 1
+        return "PS%d" % ((6 + xb[0] % 2) if xb[0] < NB else xb[0] % 4)
+
+    peers = [q for q in range(NR) if q != rank]
+
+    def send(k, src, land, width, at):
+        mask = topo.mask(T.cores[rank], T.cores[peers[0]])
+        per = len(topo.engines(T.cores[rank], T.cores[peers[0]]))
+
+        def fn():
+            ids, dsts = [], []
+            for q in peers:
+                rid, pid, _ = topo.addr(T.cores[q])
+                a = width * [x for x in range(NR) if x != q].index(rank) + at
+                ids.append(DstId(rid=rid, pnc=pid))
+                dsts.append(T[land][:, a:a + 1024])
+            tr = RemoteDMATransfer(dst_ids=ids, dma_engine_mask=mask, remote_sem=T.sem["ar%d" % (3 * rank + k)],
+                                   src=src[0], dsts=dsts)
+            return g.remote_dma_fused([tr], local_sem=T.sem.sent)
+        i = add("G", fn, 3 * 128 * 2048 / RATE, src[1], [], "r")
+        for s, q in enumerate(peers):
+            j = add("X", None, 0.5, [], [(land, width * s + at, width * s + at + 1024)], "x", [i])
+            ops[j]["sem"] = (T.sem["ar%d" % (3 * q + k)], per)
+        return per
+
+    def child(r, i):
+        return 12 + r - 4 * i
+
+    npc = [0]
+
+    def unpack(a, hi, los, shift):
+        n = npc[0]
+        npc[0] += 1
+        x = 512 * (n % 4)
+        bk = xbank()
+        ts(hi, w5("LU", a), M8, M8, ALU.add, ALU.subtract)
+        w = 512 // len(los)
+        if ROUTE[n] == "P":
+            cp(w5("X32", x), w5("LU", a))
+            mm([(v(bk), [(df(1), w5("X32", x)), (db(-1), hi)])])
+            for i, lo in enumerate(los):
+                act(lo, w5(bk, w * i, w), shift)
+        else:
+            ts(w5("X32", x), w5("LU", a), shift, None, ALU.add)
+            mm([(v(bk), [(db(1), hi)])])
+            for i, lo in enumerate(los):
+                tt(lo, w5("X32", x + w * i, w), w5(bk, w * i, w), ALU.subtract)
+
+    nsent = 0
+    packed = []
+    for p in range(2):
+        bk = xbank()
+        mm([(v(bk), [(db(256), w5("RM0", 512 * p)), (db(1), w5("NR0", 1024 + 512 * p))])])
+        packed.append(cp(w5("XU", 512 * p), v(bk)))
+    nsent += send(0, w5("XU", 0, 1024), "LU", 2048, 0)
+    n1 = ts(v("N1", 4096, 5120), v("NR0", 1024, 2048), -32.0, None, ALU.add)
+    ops[n1]["deps"] |= set(packed)
+    loads([("KD", T.kid, 0, B), ("RM0", T.room, 1024, 2048)], [n1])
+    ts(v("N1", 3072, 4096), v("NR0", 0, 1024), -32.0, None, ALU.add)
+    for p in range(2):
+        bk = xbank()
+        mm([(w5(bk, 256 * i, 256), [(db(64), v("WT", child(rank, 2 * p + i), B, 16)), (db(1), w5("NR0", 512 * p + 256 * i, 256))])
+            for i in (0, 1)])
+        ts(w5("XH", 512 * p), v(bk), -2048.0, None, ALU.add)
+    nsent += send(1, v("XH"), "LH", 1024, 0)
+    cur[0] = -2
+    for s, q in enumerate(peers):
+        for p in range(2):
+            unpack(2048 * s + 512 * p, w5("R2", D * q + 512 * p), [w5("N2", H * (3 - q) + 1024 + 512 * p)], -32.0)
+    cur[0] = -1
+    for i in range(4):
+        act(w5("SN", 256 * i, 256), v("KD", child(rank, i), B, 16), -127.5, 1.0, AF.Sign)
+    for p in range(2):
+        bk = xbank()
+        mm([(w5(bk, 256 * i, 256), [(db(256), w5("RM0", 1024 + 512 * p + 256 * i, 256)), (db(1), v("KD", child(rank, 2 * p + i), B, 16)),
+                                    (db(-64), w5("SN", 512 * p + 256 * i, 256))]) for i in (0, 1)])
+        ts(w5("XU", 1024 + 512 * p), v(bk), -64.0, None, ALU.add)
+    nsent += send(2, w5("XU", 1024, 1024), "LU", 2048, 1024)
+    for p in range(4):
+        act(w5("N2", H * (3 - rank) + 512 * p), w5("NR0", 512 * p), -32.0)
+        act(w5("R2", D * rank + 512 * p), w5("RM0", 512 * p), 0.0, 256.0)
+        act(w5("W2", 256 * (15 - child(rank, p)), 256), v("WT", child(rank, p), B, 16), 129.0)
+    for p in range(2):
+        bk = xbank()
+        mm([(w5(bk, 256 * i, 256), [(db(1), v("KD", child(rank, 2 * p + i), B, 16)), (db(-64), w5("SN", 512 * p + 256 * i, 256))])
+            for i in (0, 1)])
+        for i in (0, 1):
+            act(w5("K2", 256 * (15 - child(rank, 2 * p + i)), 256), w5(bk, 256 * i, 256), -64.0)
+
+    def second():
+        for s, q in enumerate(peers):
+            for p in range(2):
+                bk = xbank()
+                gr = []
+                for i in (0, 1):
+                    hi, y = w5("W2", 256 * (15 - child(q, 2 * p + i)), 256), w5("LH", 1024 * s + 512 * p + 256 * i, 256)
+                    ts(hi, y, 1 / 64, 161 - 31.5 / 64, ALU.mult, ALU.add)
+                    gr.append((w5(bk, 256 * i, 256), [(dh(1), y), (db(-64), hi)]))
+                mm(gr)
+                act(w5("N2", H * (3 - q) + 512 * p), v(bk), 10272.0)
+        for s, q in enumerate(peers):
+            for p in range(2):
+                unpack(2048 * s + 1024 + 512 * p, w5("R2", D * q + 1024 + 512 * p),
+                       [w5("K2", 256 * (15 - child(q, 2 * p + i)), 256) for i in (0, 1)], 0.0)
+        late = [j for j, o in enumerate(ops) if o["kind"] == "x"][-3:]
+        dma(T.ND0[:], T.need[:], 128 * O * 2, [], [("ND0", 0, O)], late)
+        for name, src in (("WT", T.wt), ("KD", T.kid)):
+            dma(v(name, B, 2 * B)[0], src[:], 128 * B * 2, [], [(name, B, 2 * B)], late)
+        dma(v("N1", 1024, 3072)[0], v("N1", 3072, 5120)[0], 128 * 4096, [("N1", 3072, 5120)], [("N1", 1024, 3072)], late)
+        dma(v("N1", 0, 1024)[0], v("N1", 4096, 5120)[0], 128 * 2048, [("N1", 4096, 5120)], [("N1", 0, 1024)], late)
+        for name, src in (("WT", T.wt), ("KD", T.kid)):
+            dma(v(name, 2 * B, WTW)[0], src[:, 0:WTW - 2 * B], 128 * 1728, [], [(name, 2 * B, WTW)], late)
+        if "V" in ROOM_ON:
+            for p in range(4):
+                act(w5("ND1", 512 * p), w5("ND0", 512 * p), 0.0, 256.0)
+
+    def L(name, c, base=0):
+        return v(name, base + c * CW, base + (c + 1) * CW)
+
+    def sm(c, k):
+        per = 512 // (8 * CW)
+        a = (c % per) * 8 * CW + k * CW
+        return v("PS%d" % (4 + c // per), a, a + CW)
+
+    def kbank(c, i):
+        return "PS%d" % (c * (NO // 512) + i)
+
+    def draw(c, wwin, wbias, kwin, nwin, ob, oh):
+        o0 = c * NO
+        for i in range(NO // 512):
+            a, k0 = o0 + 512 * i, c * CW + 32 * i
+            act(w5("GA", a), ind(wwin, w5(ob, k0, 32)), wbias)
+            tt(w5("GP", a), ind(nwin, w5(oh, k0, 32)), w5("GA", a), ALU.mult)
+        for i in range(NO // 512):
+            act(w5("GK", o0 + 512 * i), ind(kwin, w5(ob, c * CW + 32 * i, 32)))
+        for i in range(NO // 512):
+            bk = kbank(c, i)
+            mm([(w5(bk, 128 * j, 128),
+                 [(v("GP", o0 + 4 * i + j, o0 + NO, S), dh(4096)), (v("GA", o0 + 4 * i + j, o0 + NO, S), db(2 ** 17)),
+                  (v("GK", o0 + 4 * i + j, o0 + NO, S), db(1))]) for j in range(4)])
+            scan(w5("SC", c * SW + 512 * i), v("DL"), v(bk), ALU.add, ALU.max)
+        act(w5("QB", c * QW + 16, 128), ind(w5("SC", c * SW, SW), v("OQ")), KBIAS)
+        mm([(sm(c, 0), [(w5("QB", c * QW + 16 - S * k, 128), w5("EE", k * CW, CW)) for k in range(NSH)])])
+        ts(L("HH", c), sm(c, 0), M12, M12, ALU.add, ALU.subtract)
+        tt(L("QC", c), sm(c, 0), L("HH", c), ALU.subtract)
+
+    CD = 32760 + 4097 * 160 + 15 - 477 * 2048
+    for rd in range(RO):
+        for c in range(NC):
+            cur[0] = c
+            if rd == 0:
+                draw(c, v("WT", 0, B), 0.0, v("KD", 0, B), v("N1", 3072, 5120), "OB", "OH")
+            else:
+                w = 6576 if rd == 1 else WTW
+                draw(c, v("WT", 0, w), 0.0, v("KD", 0, w), v("N1"), "OB", "OH")
+            ts(L("OB2", c), L("QC", c), 2047.5, None, ALU.add)
+            act(L("CP", c), L("QC", c), 167.5, 1 / 256)
+            act(L("UP", c), L("QC", c), 161.5, 1 / 1024)
+            base = [(df(592), L("QC", c)), (dh(1), L("BS", c))]
+            if rd:
+                base.append((dh(611), L("TT", c, 128 * (rd - 1))))
+            mm([(sm(c, 1), base + [(db(-37), L("CP", c))]),
+                (sm(c, 2), base + [(dh(2011), L("CP", c)), (db(-8192), L("UP", c))])])
+            ts(L("H2", c), sm(c, 1), M11, M11, ALU.add, ALU.subtract)
+            tt(L("T2", c), sm(c, 2), L("H2", c), ALU.subtract)
+            ts(L("OH2", c), L("T2", c), 1023.5 + 983040, None, ALU.add)
+            mm([(sm(c, 3), [(db(1), L("CP", c)), (db(-4), L("UP", c))] + ([(db(8), L("BO", c))] if rd == 2 else []))])
+            a = 4 * CW * c
+            for k in range(4):
+                ts(w5("MK", a + CW * k, CW), sm(c, 3), float(k - 480), None, ALU.is_equal)
+            if c == 0:
+                scan(w5("IK", 0, 4 * CW), w5("RS", 0, 4 * CW), w5("MK", 0, 4 * CW), ALU.mult, ALU.add)
+            else:
+                for k in range(4):
+                    b = a + CW * k
+                    scan(w5("IK", b, CW), w5("RS", 4 * CW, CW), w5("MK", b, CW), ALU.mult, ALU.add, w5("IK", b - 3 * CW - 1, 1))
+            mm([(w5("PS6", a, 4 * CW), [(v("BLK"), w5("IK", a, 4 * CW)), (v("UT"), w5("MK", a, 4 * CW))])])
+            act(w5("SG", a, 4 * CW), w5("PS6", a, 4 * CW), CAP + 0.5 - 4096, -1.0, AF.Sign)
+            mm([(L("PS7", c), [(db(1), w5("SG", a + CW * k, CW)) for k in range(4)])])
+            act(L("GS", c), L("PS7", c))
+        if rd == 0:
+            cur[0] = -2
+            second()
+        for c in range(NC):
+            cur[0] = c
+            o0 = c * NO
+            draw(c, v("W2"), -129.0, v("K2"), v("N2"), "OB2", "OH2")
+            act(L("CP2", c), L("QC", c), 167.5, 1 / 256)
+            mm([(sm(c, 4), [(df(16), L("QC", c)), (db(-2048), L("CP", c)), (db(8192), L("UP", c)),
+                            (db(-4096), L("CP2", c)), (db(-1), L("CP2", c))])])
+            ts(L("OR", c), sm(c, 4), float(CD), None, ALU.add)
+            act(L("DV", c), sm(c, 4), CD + 1)
+            for i in range(NO // 512):
+                a = o0 + 512 * i
+                gi = ind(v("R2"), w5("OR", c * CW + 32 * i, 32))
+                if ROOM_ON[rd * NC + c] == "A":
+                    act(w5("GR", a), gi)
+                    mm([(v(kbank(c, i)), [(db(256), w5("ND0", a)), (db(-1), w5("GR", a))])])
+                    act(w5("VI", a), v(kbank(c, i)), 0.0, 1.0, AF.Relu)
+                else:
+                    tt(w5("VI", a), gi, w5("ND1", a), ALU.is_lt)
+            terms = [(db(-1), L("GS", c))]
+            if rd:
+                tt(L("EQ", c), L("DV", c), L("KV", c) if rd == 1 else L("S12", c), ALU.is_equal)
+                terms.append((db(1), L("EQ", c)))
+            if rd == 2:
+                tt(L("DA", c), L("DV", c), L("NN", c), ALU.mult)
+                tt(L("DBB", c), L("DV", c), L("DA", c), ALU.subtract)
+            terms += [(w5("SEL", 15 - r, 128), v("VI", o0 + r, o0 + NO, 16)) for r in range(16)]
+            mm([(sm(c, 5), terms)])
+            kp = L("KP", c, 128 * rd)
+            ts(kp, sm(c, 5), 2.5, None, ALU.is_le)
+            if rd < 2:
+                up = ([L("TT", c)] if rd else []) + [L("GS", c)]
+                mm([(sm(c, 6), [(dh(1), L("BB", c))] + [(dh(1237), x) for x in up] + [(dh(-1237), kp)]),
+                    (sm(c, 7), [(dh(1), L("BA", c))] + [(dh(-724), x) for x in up] + [(dh(724), kp)])])
+                ts(L("OB", c), sm(c, 6), 2048.0 + 4 * 1237, None, ALU.add)
+                ts(L("OH", c), sm(c, 7), 1024.0 - 4 * 724 + 3072, None, ALU.add)
+                mm([(L("PS7", c, 128), [(db(1), x) for x in up] + [(db(-1), kp)])])
+                act(L("TT", c, 128 * rd), L("PS7", c, 128), 4.0)
+                tt(L("KV", c, 128 * rd), kp, L("DV", c), ALU.mult)
+            if rd == 1:
+                tt(L("BO", c), L("KP", c), kp, ALU.mult)
+                tt(L("S12", c), L("KV", c), L("KV", c, 128), ALU.add)
+                tt(L("U1", c), L("KP", c), L("KV", c, 128), ALU.mult)
+                tt(L("U2", c), L("S12", c), L("U1", c), ALU.subtract)
+                act(L("B12", c), L("U1", c), -1.0)
+                act(L("A12", c), L("U2", c), -1.0)
+                ts(L("NN", c), L("S12", c), 0.0, None, ALU.is_equal)
+            if rd == 2:
+                for y, dst, dv, old, tmp in (("YA", T.ya, "DA", "A12", "U1"), ("YB", T.yb, "DBB", "B12", "U2")):
+                    tt(L(tmp, c), kp, L(dv, c), ALU.mult)
+                    tt(L(y, c), L(tmp, c), L(old, c), ALU.add)
+                    dma(dst[:, c * CW:(c + 1) * CW], L(y, c)[0], 128 * CW * 4, L(y, c)[1], [])
+    return ops, nsent
+
+
+def plan(ops, succ, prio):
+    n = len(ops)
+    left = [len(o["deps"]) + len(o.get("after", [])) for o in ops]
+    ready = [i for i in range(n) if left[i] == 0]
+    fin, dep, free, pipe, last, order, more = [0.0] * n, [0.0] * n, {}, 0.0, {}, [], {}
+    while ready:
+        st = {}
+        for i in ready:
+            o = ops[i]
+            t = max(free.get(o["q"], 0.0), dep[i])
+            for b in o["banks"]:
+                for q, j in last.get(b, {}).items():
+                    if q != o["q"]:
+                        t = max(t, fin[j] + LAT_X)
+            st[i] = t
+        i0 = min(ready, key=st.get)
+        i = max([k for k in ready if ops[k]["q"] == ops[i0]["q"] and st[k] <= st[i0] + SLACK], key=lambda k: prio[k])
+        o = ops[i]
+        for b in o["banks"]:
+            for q, j in last.get(b, {}).items():
+                if q != o["q"]:
+                    more.setdefault(i, set()).add(j)
+            last.setdefault(b, {})[o["q"]] = i
+        if o["kind"] in "dr":
+            free[o["q"]] = st[i] + (0.1 if o["kind"] == "d" else 1.0)
+            pipe = max(pipe, st[i] + 1.5) + o["dur"]
+            fin[i] = pipe
+        elif o["kind"] == "x":
+            fin[i] = st[i] + o["dur"]
+        else:
+            fin[i] = free[o["q"]] = st[i] + o["dur"]
+        order.append(i)
+        ready.remove(i)
+        for j in succ[i]:
+            left[j] -= 1
+            if i in ops[j]["deps"]:
+                dep[j] = max(dep[j], fin[i] + (LAT_S if ops[j]["q"] == o["q"] else LAT_X))
+            if left[j] == 0:
+                ready.append(j)
+    return max(fin), order, more
+
+
+CACHE = {}
+
+
+def schedule(ops):
+    n = len(ops)
+    succ = [[] for _ in ops]
+    for i, o in enumerate(ops):
+        for d in list(o["deps"]) + o.get("after", []):
+            succ[d].append(i)
+    if "prio" not in CACHE:
+        prio = [0.0] * n
+        for i in range(n - 1, -1, -1):
+            prio[i] = ops[i]["dur"] + (1.5 if ops[i]["kind"] in "dr" else LAT_X) + max([prio[j] for j in succ[i]] + [0.0])
+        prio = np.array([p + {-1: PRE, -2: PRE2}.get(o["c"], -SKEW * o["c"]) for p, o in zip(prio, ops)])
+        rng = np.random.default_rng(1)
+        best = plan(ops, succ, prio)[0]
+        for _ in range(TUNE):
+            a, w = int(rng.integers(0, n)), int(rng.integers(1, 40))
+            p = prio.copy()
+            p[a:a + w] += SIGMA * rng.normal() + 0.3 * SIGMA * rng.normal(size=len(p[a:a + w]))
+            t = plan(ops, succ, p)[0]
+            if t <= best:
+                best, prio = t, p
+        CACHE["prio"] = prio
+    _, order, more = plan(ops, succ, CACHE["prio"])
+    for i, m in more.items():
+        ops[i]["deps"] |= m
+    return order
+
+
+def rank_program(g, core, T, topo):
+    rank = T.rank_of(core)
+    if rank is None:
+        return
+    ops, nsent = build(g, T, topo, rank)
+    order = schedule(ops)
+    eng = {"V": g.vector, "A": g.scalar, "P": g.tensor, "G": g, "S": g.sync}
+    cnt = {"V": 0, "A": 0, "P": 0, "G": 0}
+    seen = {}
+    for i in order:
+        o = ops[i]
+        if o["kind"] == "x":
+            continue
+        need = {}
+        for d in o["deps"]:
+            p = ops[d]
+            if p["kind"] == "c":
+                key = "c" + p["q"]
+                need[key] = (T.sem[key], max(p["n"], need.get(key, (0, 0))[1]))
+            else:
+                need["op%d" % d] = p["sem"]
+        for key, (sem, val) in need.items():
+            if seen.get((o["q"], key), 0) < val:
+                eng[o["q"]].wait_ge(sem, val)
+                seen[(o["q"], key)] = val
+        ins = o["fn"]()
+        if o["kind"] == "c":
+            cnt[o["q"]] += 1
+            o["n"] = cnt[o["q"]]
+            ins.then_inc(T.sem["c" + o["q"]], 1)
+        elif o["kind"] == "d":
+            ins.then_inc(o["sem"][0], 16)
+    for q in cnt:
+        g.wait_ge(T.sem["c" + q], cnt[q])
+    g.wait_ge(T.sem.sent, nsent)
+    for o in ops:
+        if o["kind"] in "dx":
+            g.wait_ge(o["sem"][0], o["sem"][1])

@@ -10,8 +10,8 @@ CW = 128 // NC
 NO = O // NC
 SW = NO + 16
 QW = 144
-ROOM_ON = "VVVVVV"
-ROUTE = "PVPVPVPVPVPV"
+ROOM_ON = "AVAVAVAVAVAV"
+ROUTE = "VVVVVVGVGVGV"
 KBIAS = -(1985 * 4096 + 2047.5)
 M12, M11, M8 = 1.5 * 2.0 ** 35, 1.5 * 2.0 ** 34, 1.5 * 2.0 ** 31
 WTW = 9056
@@ -30,7 +30,8 @@ SB = {
     "OB": (128, U16), "OH": (128, U16), "OB2": (128, U16), "OH2": (128, U16), "OR": (128, U16), "OQ": (8, U16),
     "HH": (128, F32), "QC": (128, F32), "H2": (128, F32), "T2": (128, F32),
     "CP": (128, BF), "UP": (128, BF), "CP2": (128, BF), "MK": (512, BF), "IK": (512, BF), "SG": (512, BF),
-    "RS": (512, BF), "DL": (512, BF), "GS": (128, BF), "TT": (256, BF), "KP": (384, BF), "EQ": (128, BF), "BO": (128, BF),
+    "RS": (512, BF), "DL": (512, BF), "TB": (512, BF), "GS": (128, BF), "TT": (256, BF), "KP": (384, BF),
+    "EQ": (128, BF), "BO": (128, BF),
     "DV": (128, F32), "KV": (256, F32), "S12": (128, F32), "B12": (128, F32), "A12": (128, F32), "U1": (128, F32),
     "U2": (128, F32), "NN": (128, F32), "DA": (128, F32), "DBB": (128, F32), "YA": (128, F32), "YB": (128, F32),
     "ONE": (144, F32), "EE": (NSH * CW, F32), "PI": (2, I32), "PJ": (2, I32), "PF": (2, F32),
@@ -43,10 +44,10 @@ for _i in range(8):
     SCRATCH["PS%d" % _i] = ("psum", [128, 512], F32)
 SEMAPHORES = ["cV", "cA", "cP", "cG", "sent"] + ["dm%d" % i for i in range(24)] + ["ar%d" % i for i in range(12)]
 
-CY, PCY, GF = 0.83e-3 * 1.25, 0.42e-3 * 1.25, 1.56
-LAT_X, LAT_S, RATE = 0.12, 0.08, 220e3
-TUNE, SIGMA, SLACK = 1500, 1.0, 0.2
-SKEW, PRE, PRE2, NB = 4.0, 5.0, 0.0, 15
+CY, PCY, GF = 0.83e-3 * 1.1, 0.0005 * 1.1, 1.56
+LAT_X, LAT_S, RATE = 0.15, 0.1, 250e3
+TUNE, SIGMA, SLACK = 800, 1, 0.2
+SKEW, PRE, PRE2, NB = 2, 5, 0, 11
 
 
 def build(g, T, topo, rank):
@@ -80,7 +81,8 @@ def build(g, T, topo, rank):
             acc.setdefault(n, []).append((i, a, b, False))
         deps.discard(i)
         banks = set(n for (n, a, b) in reads + writes if n.startswith("PS"))
-        ops.append({"q": q, "fn": fn, "dur": dur, "deps": deps, "kind": kind, "banks": banks, "c": cur[0]})
+        ops.append({"q": q, "fn": fn, "dur": dur, "deps": deps, "kind": kind, "banks": banks, "c": cur[0],
+                    "g": int(any(n.startswith("O") and n[1] in "BHRQ" for (n, a, b) in reads))})
         return i
 
     def vcost(out, ins, tt=False):
@@ -120,7 +122,7 @@ def build(g, T, topo, rank):
         d = 0.065 + out[2] * GF * CY if len(in0) == 5 else max(64, out[2]) * CY + 0.03
         return add("A", lambda: g.scalar.activation(out[0], in0[0], func, bias=float(bias), scale=float(scale)), d, in0[1], out[1])
 
-    def mm(groups):
+    def mm(groups, first=None, end=None):
         r, w, d = [], [], 0.03
         for out, terms in groups:
             w += out[1]
@@ -132,7 +134,8 @@ def build(g, T, topo, rank):
             last = None
             for out, terms in groups:
                 for k, (l, x) in enumerate(terms):
-                    last = g.tensor.matmul(out[0], l[0], x[0], k == 0, k == len(terms) - 1)
+                    last = g.tensor.matmul(out[0], l[0], x[0], k == 0 if first is None else first,
+                                           k == len(terms) - 1 if end is None else (end and out is groups[-1][0]))
             return last
         return add("P", fn, d, r, w)
 
@@ -197,7 +200,8 @@ def build(g, T, topo, rank):
     cp(v("OQ"), v("OG"))
     asel(v("UT0"), v("BLK"), [[-1, 128]], ALU.is_gt, 0, 1)
     tt(v("UT"), db(-4096), v("UT0"), ALU.subtract)
-    ms(v("DL"), 256.0)
+    ms(v("DL"), 0.0)
+    iota(v("TB"), [[0, 32], [-256, 16]], 3840, 0)
     ms(v("DL", 0, 512, 16), -2.0 ** 24)
     ms(v("RS"), 1.0)
     ms(v("RS", 0, 3 * CW + 1, CW), 0.0)
@@ -256,8 +260,8 @@ def build(g, T, topo, rank):
         bk = xbank()
         ts(hi, w5("LU", a), M8, M8, ALU.add, ALU.subtract)
         w = 512 // len(los)
-        if ROUTE[n] == "P":
-            cp(w5("X32", x), w5("LU", a))
+        if ROUTE[n] == "G":
+            asel(w5("X32", x), w5("LU", a), [[0, 512]], ALU.is_ge, 0, 0)
             mm([(v(bk), [(df(1), w5("X32", x)), (db(-1), hi)])])
             for i, lo in enumerate(los):
                 act(lo, w5(bk, w * i, w), shift)
@@ -274,10 +278,10 @@ def build(g, T, topo, rank):
         mm([(v(bk), [(db(256), w5("RM0", 512 * p)), (db(1), w5("NR0", 1024 + 512 * p))])])
         packed.append(cp(w5("XU", 512 * p), v(bk)))
     nsent += send(0, w5("XU", 0, 1024), "LU", 2048, 0)
-    n1 = ts(v("N1", 4096, 5120), v("NR0", 1024, 2048), -32.0, None, ALU.add)
+    n1 = act(w5("N2", H * (3 - rank) + 1024, 1024), v("NR0", 1024, 2048), -32.0)
     ops[n1]["deps"] |= set(packed)
     loads([("KD", T.kid, 0, B), ("RM0", T.room, 1024, 2048)], [n1])
-    ts(v("N1", 3072, 4096), v("NR0", 0, 1024), -32.0, None, ALU.add)
+    act(w5("N2", H * (3 - rank), 1024), v("NR0", 0, 1024), -32.0)
     for p in range(2):
         bk = xbank()
         mm([(w5(bk, 256 * i, 256), [(db(64), v("WT", child(rank, 2 * p + i), B, 16)), (db(1), w5("NR0", 512 * p + 256 * i, 256))])
@@ -292,17 +296,16 @@ def build(g, T, topo, rank):
     for i in range(4):
         act(w5("SN", 256 * i, 256), v("KD", child(rank, i), B, 16), -127.5, 1.0, AF.Sign)
     for p in range(2):
-        bk = xbank()
+        bk = "PS%d" % (4 + p)
         mm([(w5(bk, 256 * i, 256), [(db(256), w5("RM0", 1024 + 512 * p + 256 * i, 256)), (db(1), v("KD", child(rank, 2 * p + i), B, 16)),
                                     (db(-64), w5("SN", 512 * p + 256 * i, 256))]) for i in (0, 1)])
         ts(w5("XU", 1024 + 512 * p), v(bk), -64.0, None, ALU.add)
     nsent += send(2, w5("XU", 1024, 1024), "LU", 2048, 1024)
     for p in range(4):
-        act(w5("N2", H * (3 - rank) + 512 * p), w5("NR0", 512 * p), -32.0)
         act(w5("R2", D * rank + 512 * p), w5("RM0", 512 * p), 0.0, 256.0)
         act(w5("W2", 256 * (15 - child(rank, p)), 256), v("WT", child(rank, p), B, 16), 129.0)
     for p in range(2):
-        bk = xbank()
+        bk = "PS%d" % (4 + p)
         mm([(w5(bk, 256 * i, 256), [(db(1), v("KD", child(rank, 2 * p + i), B, 16)), (db(-64), w5("SN", 512 * p + 256 * i, 256))])
             for i in (0, 1)])
         for i in (0, 1):
@@ -327,8 +330,9 @@ def build(g, T, topo, rank):
         dma(T.ND0[:], T.need[:], 128 * O * 2, [], [("ND0", 0, O)], late)
         for name, src in (("WT", T.wt), ("KD", T.kid)):
             dma(v(name, B, 2 * B)[0], src[:], 128 * B * 2, [], [(name, B, 2 * B)], late)
-        dma(v("N1", 1024, 3072)[0], v("N1", 3072, 5120)[0], 128 * 4096, [("N1", 3072, 5120)], [("N1", 1024, 3072)], late)
-        dma(v("N1", 0, 1024)[0], v("N1", 4096, 5120)[0], 128 * 2048, [("N1", 4096, 5120)], [("N1", 0, 1024)], late)
+        for a, b, n in ((3072, 0, H), (1024, 0, H), (0, 1024, 1024)):
+            src = w5("N2", H * (3 - rank) + b, n)
+            dma(w5("N1", a, n)[0], src[0], 256 * n, src[1], w5("N1", a, n)[1], late)
         for name, src in (("WT", T.wt), ("KD", T.kid)):
             dma(v(name, 2 * B, WTW)[0], src[:, 0:WTW - 2 * B], 128 * 1728, [], [(name, 2 * B, WTW)], late)
         if "V" in ROOM_ON:
@@ -356,9 +360,10 @@ def build(g, T, topo, rank):
             act(w5("GK", o0 + 512 * i), ind(kwin, w5(ob, c * CW + 32 * i, 32)))
         for i in range(NO // 512):
             bk = kbank(c, i)
-            mm([(w5(bk, 128 * j, 128),
-                 [(v("GP", o0 + 4 * i + j, o0 + NO, S), dh(4096)), (v("GA", o0 + 4 * i + j, o0 + NO, S), db(2 ** 17)),
-                  (v("GK", o0 + 4 * i + j, o0 + NO, S), db(1))]) for j in range(4)])
+            mm([(v(bk), [(db(1), v("TB"))])], True, False)
+            mm([(w5(bk, 128 * j, 128), [(v("GP", o0 + 4 * i + j, o0 + NO, S), dh(4096)),
+                                        (v("GA", o0 + 4 * i + j, o0 + NO, S), db(2 ** 17))]) for j in range(4)], False, False)
+            mm([(w5(bk, 128 * j, 128), [(v("GK", o0 + 4 * i + j, o0 + NO, S), db(1))]) for j in range(4)], False, True)
             scan(w5("SC", c * SW + 512 * i), v("DL"), v(bk), ALU.add, ALU.max)
         act(w5("QB", c * QW + 16, 128), ind(w5("SC", c * SW, SW), v("OQ")), KBIAS)
         mm([(sm(c, 0), [(w5("QB", c * QW + 16 - S * k, 128), w5("EE", k * CW, CW)) for k in range(NSH)])])
@@ -370,7 +375,7 @@ def build(g, T, topo, rank):
         for c in range(NC):
             cur[0] = c
             if rd == 0:
-                draw(c, v("WT", 0, B), 0.0, v("KD", 0, B), v("N1", 3072, 5120), "OB", "OH")
+                draw(c, v("WT", 0, B), 0.0, v("KD", 0, B), w5("N2", H * (3 - rank), H), "OB", "OH")
             else:
                 w = 6576 if rd == 1 else WTW
                 draw(c, v("WT", 0, w), 0.0, v("KD", 0, w), v("N1"), "OB", "OH")
@@ -414,7 +419,7 @@ def build(g, T, topo, rank):
             for i in range(NO // 512):
                 a = o0 + 512 * i
                 gi = ind(v("R2"), w5("OR", c * CW + 32 * i, 32))
-                if ROOM_ON[rd * NC + c] == "A":
+                if ROOM_ON[(rd * NC + c) * 2 + i] == "A":
                     act(w5("GR", a), gi)
                     mm([(v(kbank(c, i)), [(db(256), w5("ND0", a)), (db(-1), w5("GR", a))])])
                     act(w5("VI", a), v(kbank(c, i)), 0.0, 1.0, AF.Relu)
@@ -498,6 +503,28 @@ def plan(ops, succ, prio):
     return max(fin), order, more
 
 
+def replay(ops, order, more, m):
+    fin, free, pipe = [0.0] * len(ops), {}, 0.0
+    for i in order:
+        o = ops[i]
+        t = free.get(o["q"], 0.0)
+        for d in o["deps"]:
+            t = max(t, fin[d] + m[3])
+        for d in more.get(i, ()):
+            t = max(t, fin[d] + m[3])
+        if o["kind"] in "dr":
+            free[o["q"]] = t + (0.1 if o["kind"] == "d" else 1.0)
+            pipe = fin[i] = max(pipe, t + 1.5) + o["dur"] * m[4 if o["kind"] == "d" else 5]
+        elif o["kind"] == "x":
+            fin[i] = t + o["dur"]
+        else:
+            fin[i] = free[o["q"]] = t + o["dur"] * m[2 if o["q"] == "P" else o["g"]]
+    return max(fin)
+
+
+CASES = [(0.92, 0.92, 1.05, 0.1, 0.83, 0.83), (0.92, 0.92, 0.85, 0.15, 0.83, 1.6), (1.27, 1.6, 1.1, 0.06, 0.83, 0.83),
+         (1.36, 1.05, 1.3, 0.12, 1.2, 1.2)]
+SEED, HEAT = 1, 0.0
 CACHE = {}
 
 
@@ -512,15 +539,19 @@ def schedule(ops):
         for i in range(n - 1, -1, -1):
             prio[i] = ops[i]["dur"] + (1.5 if ops[i]["kind"] in "dr" else LAT_X) + max([prio[j] for j in succ[i]] + [0.0])
         prio = np.array([p + {-1: PRE, -2: PRE2}.get(o["c"], -SKEW * o["c"]) for p, o in zip(prio, ops)])
-        rng = np.random.default_rng(1)
-        best = plan(ops, succ, prio)[0]
-        for _ in range(TUNE):
-            a, w = int(rng.integers(0, n)), int(rng.integers(1, 40))
+        rng = np.random.default_rng(SEED)
+        base = None
+        for it in range(TUNE + 1):
             p = prio.copy()
-            p[a:a + w] += SIGMA * rng.normal() + 0.3 * SIGMA * rng.normal(size=len(p[a:a + w]))
-            t = plan(ops, succ, p)[0]
-            if t <= best:
-                best, prio = t, p
+            if it:
+                a, w = int(rng.integers(0, n)), int(rng.integers(1, 30))
+                p[a:a + w] += SIGMA * rng.normal() + 0.5 * SIGMA * rng.normal(size=len(p[a:a + w]))
+            _, order, more = plan(ops, succ, p)
+            t = np.array([replay(ops, order, more, m) for m in CASES])
+            if base is None:
+                base, best = t, 1.0
+            if (t / base).mean() <= best + HEAT * (1 - it / TUNE) * rng.random():
+                best, prio = (t / base).mean(), p
         CACHE["prio"] = prio
     _, order, more = plan(ops, succ, CACHE["prio"])
     for i, m in more.items():
@@ -544,6 +575,8 @@ def rank_program(g, core, T, topo):
         need = {}
         for d in o["deps"]:
             p = ops[d]
+            if p["q"] == o["q"] == "P":
+                continue
             if p["kind"] == "c":
                 key = "c" + p["q"]
                 need[key] = (T.sem[key], max(p["n"], need.get(key, (0, 0))[1]))

@@ -1,4 +1,3 @@
-import numpy as np
 from concourse.bass import DstId, RemoteDMATransfer
 from concourse.mybir import AluOpType as ALU, ActivationFunctionType as AF
 
@@ -8,33 +7,36 @@ S = 16 // NC
 NSH = 16 // S
 CW = 128 // NC
 NO = O // NC
-SW = NO + 16
 QW = 144
-ROOM_ON = "AVAVAVAVAVAV"
-ROUTE = "VVVVVVGVGVGV"
-KBIAS = -(1985 * 4096 + 2047.5)
-M12, M11, M8 = 1.5 * 2.0 ** 35, 1.5 * 2.0 ** 34, 1.5 * 2.0 ** 31
-WTW = 9056
-DB = [256, 1, 64, -64, -1, 2 ** 17, -37, -4, 8, -2048, 8192, -8192, -4096]
-DH = [4096, 1, 1237, -1237, -724, 724, 611, 2011]
-DF = [1, 592, 16]
+P = {"route": "VVVVVV",
+     "wx": "AAAAAA", "wid": "GGGGGG", "own": "GGGG", "n1": "GGGGGGGGGG",
+     "gk": "AAAAAAAAAAAA", "room": "VVVVVVVVVVVV",
+     "act": "xyzrdbnkQpP",
+     "banks": "767676012301", "split": [[0, 1], [2, 3]], "rm": 1, "nd": 1, "ps": 0}
+M9 = 1.5 * 2.0 ** 32
+WTW, WT1 = 9056, 6576
+DB = [1, -1, 64, 512, 256, 2 ** 17, 4096, 2 ** 26, 2 ** 36, 2 ** 41, -2 ** 30, -37, -4, 8,
+      -2048, 8192, -8192, -4096, -2 ** 35]
+DH = [1237, -1237, -724, 724, 611, 2011, 592, 16]
+DF = [1, 2 ** 50]
 
 BF, F16, F32, I32, U16 = "bfloat16", "float16", "float32", "int32", "uint16"
 SB = {
-    "WT": (WTW, BF), "KD": (WTW, BF), "N1": (5120, BF), "NR0": (H, BF), "RM0": (D, BF), "ND0": (O, BF), "ND1": (O, BF),
-    "W2": (B, BF), "K2": (B, BF), "N2": (NR * H, BF), "R2": (NR * D, BF), "XU": (2048, U16), "XH": (1024, F16),
-    "LU": (6144, U16), "LH": (3072, F16), "SN": (1024, BF), "X32": (2048, F32), "GA": (O, BF), "GK": (O, BF),
-    "GP": (O, F16), "GR": (O, BF), "VI": (O, BF), "SC": (NC * SW, F32), "QB": (NC * QW, F32),
+    "WT": (WTW, BF), "KD": (WTW, BF), "N1": (5120, BF), "NR0": (H, BF), "RM0": (D, BF), "ND0": (O, BF),
+    "G2": (B, F32), "N2": (NR * H, BF), "R2": (NR * D, I32), "XU": (2048, U16), "XH": (1024, F16),
+    "LU": (6144, U16), "LH": (3072, F16), "HA": (3072, F16), "X32": (3072, F32), "Y32": (1536, I32),
+    "GA": (O, BF), "GK": (O, BF), "GG": (O, F32), "GP": (O, F16), "VI": (O, BF),
+    "SC": (O, I32), "QI": (NC * 72, I32), "QB": (NC * QW, F16),
     "BEG": (128, I32), "SAL": (128, I32), "I1": (128, I32), "I2": (128, I32), "I3": (128, I32), "I4": (128, I32),
     "F1": (128, F32), "BB": (128, F16), "BA": (128, F16), "BS": (128, F16),
     "OB": (128, U16), "OH": (128, U16), "OB2": (128, U16), "OH2": (128, U16), "OR": (128, U16), "OQ": (8, U16),
-    "HH": (128, F32), "QC": (128, F32), "H2": (128, F32), "T2": (128, F32),
-    "CP": (128, BF), "UP": (128, BF), "CP2": (128, BF), "MK": (512, BF), "IK": (512, BF), "SG": (512, BF),
-    "RS": (512, BF), "DL": (512, BF), "TB": (512, BF), "GS": (128, BF), "TT": (256, BF), "KP": (384, BF),
+    "QC": (128, F16), "H2": (128, F16),
+    "CP": (128, BF), "UP": (128, BF), "CP2": (128, BF), "CQ": (128, BF), "MK": (512, BF), "IK": (512, BF), "SG": (512, BF),
+    "RS": (512, BF), "DL": (512, BF), "GS": (128, BF), "TT": (256, BF), "KP": (384, BF),
     "EQ": (128, BF), "BO": (128, BF),
     "DV": (128, F32), "KV": (256, F32), "S12": (128, F32), "B12": (128, F32), "A12": (128, F32), "U1": (128, F32),
     "U2": (128, F32), "NN": (128, F32), "DA": (128, F32), "DBB": (128, F32), "YA": (128, F32), "YB": (128, F32),
-    "ONE": (144, F32), "EE": (NSH * CW, F32), "PI": (2, I32), "PJ": (2, I32), "PF": (2, F32),
+    "ONE": (144, F32), "EE": (NSH * CW, BF), "PI": (2, I32), "PJ": (2, I32), "PF": (2, F32),
     "JF": (144, F32), "MF": (128, F32), "OF": (8, F32), "OG": (8, F32),
     "SEL": (144, BF), "BLK": (128, BF), "UT0": (128, BF), "UT": (128, BF),
     "MB": (128 * len(DB), BF), "MH": (128 * len(DH), F16), "MFF": (128 * len(DF), F32),
@@ -44,10 +46,8 @@ for _i in range(8):
     SCRATCH["PS%d" % _i] = ("psum", [128, 512], F32)
 SEMAPHORES = ["cV", "cA", "cP", "cG", "sent"] + ["dm%d" % i for i in range(24)] + ["ar%d" % i for i in range(12)]
 
-CY, PCY, GF = 0.83e-3 * 1.1, 0.0005 * 1.1, 1.56
-LAT_X, LAT_S, RATE = 0.15, 0.1, 250e3
-TUNE, SIGMA, SLACK = 800, 1, 0.2
-SKEW, PRE, PRE2, NB = 2, 5, 0, 11
+CY, PCY, GF, RATE = 0.83e-3 * 1.1, 0.0005 * 1.1, 1.56, 250e3
+ORDER = "00050B01060P0203040Q0D070I0z0y0A0a0F0b0e080c0d0H0g0p0j0G0m0L0h0i0V0U0M090n0f0C0R0T170w0v160E0K0X0W0Y131O1R0N1Q1M110Z1012140S0o150l0x0J0q0t0O0s181a0r1b1W191U1X1V0u2l1c2m2024211i2j1Z1Y1j0k2k1g1h1p1N1S1L1T1k1o1f1d1e2I2O2U2L2X2p1q1t2t25222q2u2627231y1w281r2n2o1x291v1u1z2v2r2J2a2M2K1l1m1n3x1A3v1P3u3w2R2w2s2b1s3l31362d2N3g3b1E302e2c353p3a3f3k2P323q2Q34333738393c3h3m2f3r2S3i3j2V3e3n3d2x3o1B1C1D2y2T2g3z3C1F1G1H1J1I1K3t3s3Q2h3A3U3R3S3T3F3I4f4d2W2z2Y2Z2A2i3B2C4h4l4m2E4i2B4I3y3E2D3V3D3G3O4e4g4n4K3H3J2F3P4j3W2G4o4k3L3K2H4p4L4q3N4M4Q3X4r4R4s4J4u3M4t4S4v404w4N4O3Y3Z4x4T4y4z4P414U4442434A4V4B4W45484X4Z46474H4Y4F4C50494D4E515d4a54534b5i4c555f5e5g565h4G5j5n5758595M5k5l5o5p5m5N5q5r5a5O5R5P5S5W5b525s5Q5t5u5w5c5v6o6q5x5X5T5y5U5z5Y5A5C5V5Z5B60616p6r6s6w626x6t6365676u645E5G665D5F6873715H6v6y695I756z6a6b6A6B6C79746D6e6F6E6G5J6I6H7a726L6J6K7b765K775L7c786M6N6c7d6d6T6i6U6V6f6h6j6g6O7e6P6Q7G7f6k7g6W7h7i7H7j6R6l7k7l6m7E7J6n7n7o7m7I7O7K7p7q707F6X6S7w7z7y7A7P7r7Q7L7s7t8d8f7M7u7R7x7N8e7S8g8i7T8h8n8j7U7V7W7X8P8R7C7v8o8p7Z8k8l7Y8q8081838m8T828r868Q8s6Z7B6Y7D8t8u8w8U8X8y8S8v8x87848z8V9n9p8C8A8Y8Z9r9v9s858W8B8F8E888D9o9q90918G9t929w939x8K9u948H8I969y95978998998J9z9b9d9A9B9C9c9E9a8a8b9D8c9F9G9H8L8M8N8O9f9g9I9K9J9N9O9e9h9k9L9i9M9l9S9P9T9Q9j9m9U9R"
 
 
 def build(g, T, topo, rank):
@@ -122,8 +122,13 @@ def build(g, T, topo, rank):
         d = 0.065 + out[2] * GF * CY if len(in0) == 5 else max(64, out[2]) * CY + 0.03
         return add("A", lambda: g.scalar.activation(out[0], in0[0], func, bias=float(bias), scale=float(scale)), d, in0[1], out[1])
 
-    def mm(groups, first=None, end=None):
-        r, w, d = [], [], 0.03
+    def lin(tag, out, in0, scale, bias):
+        if tag in P["act"]:
+            return act(out, in0, bias, scale)
+        return ts(out, in0, float(scale), float(bias), ALU.mult, ALU.add)
+
+    def mm(groups, first=None, end=None, more=()):
+        r, w, d = [], list(more), 0.03
         for out, terms in groups:
             w += out[1]
             for l, x in terms:
@@ -132,10 +137,10 @@ def build(g, T, topo, rank):
 
         def fn():
             last = None
-            for out, terms in groups:
+            for n, (out, terms) in enumerate(groups):
                 for k, (l, x) in enumerate(terms):
-                    last = g.tensor.matmul(out[0], l[0], x[0], k == 0 if first is None else first,
-                                           k == len(terms) - 1 if end is None else (end and out is groups[-1][0]))
+                    last = g.tensor.matmul(out[0], l[0], x[0], k == 0 if first is None else (first and n == k == 0),
+                                           k == len(terms) - 1 and (end is None or (end and n == len(groups) - 1)))
             return last
         return add("P", fn, d, r, w)
 
@@ -145,6 +150,9 @@ def build(g, T, topo, rank):
 
     def asel(out, in0, pat, op, base, mult):
         return add("G", lambda: g.affine_select(out[0], in0[0], pat, op, 0.0, base, mult), 0.17 + 2 * out[2] * CY, in0[1], out[1])
+
+    def widen(out, in0, on="G"):
+        return asel(out, in0, [[0, out[2]]], ALU.is_ge, 0, 0) if on == "G" else act(out, in0) if on == "A" else cp(out, in0)
 
     nd = [0]
 
@@ -169,17 +177,17 @@ def build(g, T, topo, rank):
     prev = []
 
     def loads(lst, extra=()):
-        for name, src, a, b in lst:
-            i = dma(v(name, a, b)[0], src[:, a:b], 128 * (b - a) * (4 if b == 128 else 2), [], [(name, a, b)], extra)
-            ops[i]["after"] = prev[-1:]
+        for name, src, a, b, at in lst:
+            i = dma(v(name, at, at + b - a)[0], src[:, a:b], 128 * (b - a) * (4 if b == 128 else 2), [], [(name, at, at + b - a)], extra)
+            ops[i]["after"] = prev[-1:] if len(prev) < 5 else prev[4:5]
             prev.append(i)
-    loads([("NR0", T.noise, 1024, 2048), ("RM0", T.room, 0, 1024), ("BEG", T.begin, 0, 128), ("SAL", T.salt, 0, 128),
-           ("WT", T.wt, 0, B), ("NR0", T.noise, 0, 1024)])
+    loads([("NR0", T.noise, 0, H, 0), ("BEG", T.begin, 0, 128, 0), ("SAL", T.salt, 0, 128, 0), ("WT", T.wt, 0, B, 0), ("KD", T.kid, 0, B, 0)])
 
     ms(v("ONE"), 1.0)
     asel(df(1), v("ONE", 0, 128), [[-1, 128]], ALU.is_equal, 0, 1)
-    for c in DB:
-        act(db(c), df(1), 0.0, c)
+    cp(db(1), df(1))
+    for n, c in enumerate(DB[1:]):
+        lin("x" if n % 3 == 2 else "-", db(c), db(1), c, 0.0)
     for c in DH:
         ts(dh(c), db(1), float(c), None, ALU.mult)
     for c in DF[1:]:
@@ -190,43 +198,43 @@ def build(g, T, topo, rank):
     ts(v("PJ", 0, 1), v("PI", 0, 1), 112, None, ALU.bitwise_and)
     ts(v("PJ", 1, 2), v("PI", 0, 1), 15, None, ALU.bitwise_and)
     cp(v("PF", 0, 1), v("PJ", 0, 1))
-    ts(v("PF", 1, 2), v("PJ", 1, 2), 128.0, None, ALU.mult)
+    ts(v("PF", 1, 2), v("PJ", 1, 2), 8.0, None, ALU.mult)
     iota(v("JF"), [[1, 144]], -15, 0)
     iota(v("MF"), [[16, 8], [0, 16]], 0, 0)
-    iota(v("OF"), [[16, 8]], 15, 0)
+    iota(v("OF"), [[1, 8]], 0, 0)
     ts(v("SEL"), v("JF"), v("PF", 0, 1), None, ALU.is_equal)
     ts(v("BLK"), v("MF"), v("PF", 0, 1), None, ALU.is_equal)
-    ts(v("OG"), v("OF"), v("PF", 1, 2), float(NO), ALU.add, ALU.min)
+    ts(v("OG"), v("OF"), v("PF", 1, 2), 64.0, ALU.add, ALU.min)
     cp(v("OQ"), v("OG"))
     asel(v("UT0"), v("BLK"), [[-1, 128]], ALU.is_gt, 0, 1)
     tt(v("UT"), db(-4096), v("UT0"), ALU.subtract)
-    ms(v("DL"), 0.0)
-    iota(v("TB"), [[0, 32], [-256, 16]], 3840, 0)
+    ms(v("DL"), 256.0)
     ms(v("DL", 0, 512, 16), -2.0 ** 24)
     ms(v("RS"), 1.0)
     ms(v("RS", 0, 3 * CW + 1, CW), 0.0)
     ms(v("QB"), 0.0)
     for c in range(NC):
-        ms(v("SC", c * SW + NO, (c + 1) * SW), -KBIAS)
+        ms(v("QI", 72 * c + 64, 72 * c + 72), 2048)
 
-    cp(v("OB"), v("BEG"))
-    ts(v("F1"), v("BEG"), 37.0, None, ALU.mult)
+    widen(v("OB"), v("BEG"), "A")
+    act(v("F1"), v("BEG"), 0.0, 37.0)
     tt(v("I1"), v("F1"), v("SAL"), ALU.add)
     ts(v("I2"), v("I1"), H - 1, None, ALU.bitwise_and)
     cp(v("OH"), v("I2"))
-    ts(v("BB"), v("BEG"), -2048.0, None, ALU.add)
-    ts(v("BA"), v("I2"), -1024.0, None, ALU.add)
-    ts(v("I3"), v("SAL"), 35.0, None, ALU.add)
+    act(v("BB"), v("BEG"), -2048.0)
+    act(v("BA"), v("I2"), -1024.0)
+    act(v("I3"), v("SAL"), 331.0)
     ts(v("I4"), v("I3"), H - 1, None, ALU.bitwise_and)
-    ts(v("BS"), v("I4"), -1023.5, None, ALU.add)
+    act(v("BS"), v("I4"), -1023.5)
 
     xb = [0]
 
     def xbank():
         xb[0] += 1
-        return "PS%d" % ((6 + xb[0] % 2) if xb[0] < NB else xb[0] % 4)
+        return "PS" + P["banks"][(xb[0] - 1) % len(P["banks"])]
 
     peers = [q for q in range(NR) if q != rank]
+    came = []
 
     def send(k, src, land, width, at):
         mask = topo.mask(T.cores[rank], T.cores[peers[0]])
@@ -246,185 +254,173 @@ def build(g, T, topo, rank):
         for s, q in enumerate(peers):
             j = add("X", None, 0.5, [], [(land, width * s + at, width * s + at + 1024)], "x", [i])
             ops[j]["sem"] = (T.sem["ar%d" % (3 * q + k)], per)
+        came.append(j)
         return per
 
     def child(r, i):
         return 12 + r - 4 * i
 
-    npc = [0]
+    def mine(name, i):
+        return v(name, child(rank, i), B, 16)
 
-    def unpack(a, hi, los, shift):
-        n = npc[0]
-        npc[0] += 1
-        x = 512 * (n % 4)
-        bk = xbank()
-        ts(hi, w5("LU", a), M8, M8, ALU.add, ALU.subtract)
-        w = 512 // len(los)
-        if ROUTE[n] == "G":
-            asel(w5("X32", x), w5("LU", a), [[0, 512]], ALU.is_ge, 0, 0)
-            mm([(v(bk), [(df(1), w5("X32", x)), (db(-1), hi)])])
-            for i, lo in enumerate(los):
-                act(lo, w5(bk, w * i, w), shift)
-        else:
-            ts(w5("X32", x), w5("LU", a), shift, None, ALU.add)
-            mm([(v(bk), [(db(1), hi)])])
-            for i, lo in enumerate(los):
-                tt(lo, w5("X32", x + w * i, w), w5(bk, w * i, w), ALU.subtract)
-
-    nsent = 0
-    packed = []
+    own = H * (3 - rank)
     for p in range(2):
-        bk = xbank()
-        mm([(v(bk), [(db(256), w5("RM0", 512 * p)), (db(1), w5("NR0", 1024 + 512 * p))])])
-        packed.append(cp(w5("XU", 512 * p), v(bk)))
-    nsent += send(0, w5("XU", 0, 1024), "LU", 2048, 0)
-    n1 = act(w5("N2", H * (3 - rank) + 1024, 1024), v("NR0", 1024, 2048), -32.0)
-    ops[n1]["deps"] |= set(packed)
-    loads([("KD", T.kid, 0, B), ("RM0", T.room, 1024, 2048)], [n1])
-    act(w5("N2", H * (3 - rank), 1024), v("NR0", 0, 1024), -32.0)
-    for p in range(2):
-        bk = xbank()
-        mm([(w5(bk, 256 * i, 256), [(db(64), v("WT", child(rank, 2 * p + i), B, 16)), (db(1), w5("NR0", 512 * p + 256 * i, 256))])
-            for i in (0, 1)])
-        ts(w5("XH", 512 * p), v(bk), -2048.0, None, ALU.add)
-    nsent += send(1, v("XH"), "LH", 1024, 0)
-    cur[0] = -2
-    for s, q in enumerate(peers):
-        for p in range(2):
-            unpack(2048 * s + 512 * p, w5("R2", D * q + 512 * p), [w5("N2", H * (3 - q) + 1024 + 512 * p)], -32.0)
-    cur[0] = -1
-    for i in range(4):
-        act(w5("SN", 256 * i, 256), v("KD", child(rank, i), B, 16), -127.5, 1.0, AF.Sign)
+        ts(w5("N2", own + 1024 * p, 1024), w5("NR0", 1024 * p, 1024), -32.0, 512.0, ALU.add, ALU.mult)
     for p in range(2):
         bk = "PS%d" % (4 + p)
-        mm([(w5(bk, 256 * i, 256), [(db(256), w5("RM0", 1024 + 512 * p + 256 * i, 256)), (db(1), v("KD", child(rank, 2 * p + i), B, 16)),
-                                    (db(-64), w5("SN", 512 * p + 256 * i, 256))]) for i in (0, 1)])
-        ts(w5("XU", 1024 + 512 * p), v(bk), -64.0, None, ALU.add)
-    nsent += send(2, w5("XU", 1024, 1024), "LU", 2048, 1024)
-    for p in range(4):
-        act(w5("R2", D * rank + 512 * p), w5("RM0", 512 * p), 0.0, 256.0)
-        act(w5("W2", 256 * (15 - child(rank, p)), 256), v("WT", child(rank, p), B, 16), 129.0)
+        mm([(w5(bk, 256 * i, 256), [(db(64), mine("WT", 2 * p + i)), (db(1), w5("NR0", 512 * p + 256 * i, 256))]) for i in (0, 1)])
+        lin("xX"[p], w5("XH", 512 * p), v(bk), 1.0, -2048.0)
+    nsent = send(0, v("XH"), "LH", 1024, 0)
+    for p in range(2):
+        bk = "PS%d" % (6 + p)
+        mm([(w5(bk, 256 * i, 256), [(db(512), w5("NR0", 1024 + 512 * p + 256 * i, 256)), (db(1), mine("KD", 2 * p + i))]) for i in (0, 1)])
+        e = lin("yY"[p], w5("XU", 512 * p), v(bk), 1.0, 0.0)
+    nsent += send(1, w5("XU", 0, 1024), "LU", 2048, 0)
+    j = widen(w5("N1", 512 * 9, 512), w5("N2", own + 512 * 3))
+    ops[j]["after"] = [came[1] - 3]
+    loads([("RM0", T.room, 0, D, 0)], [[e], [j]][P["rm"] - 1])
     for p in range(2):
         bk = "PS%d" % (4 + p)
-        mm([(w5(bk, 256 * i, 256), [(db(1), v("KD", child(rank, 2 * p + i), B, 16)), (db(-64), w5("SN", 512 * p + 256 * i, 256))])
-            for i in (0, 1)])
+        mm([(w5(bk, 256 * i, 256), [(db(2 ** 17), mine("WT", 2 * p + i)), (db(1), mine("KD", 2 * p + i))]) for i in (0, 1)])
         for i in (0, 1):
-            act(w5("K2", 256 * (15 - child(rank, 2 * p + i)), 256), w5(bk, 256 * i, 256), -64.0)
+            act(w5("G2", 256 * (15 - child(rank, 2 * p + i)), 256), w5(bk, 256 * i, 256), 16384.0)
+    for p in range(2):
+        bk = "PS%d" % (6 + p)
+        mm([(v(bk), [(db(256), w5("RM0", 512 * p)), (db(1), w5("RM0", 1024 + 512 * p))])])
+        lin("zZ"[p], w5("XU", 1024 + 512 * p), v(bk), 1.0, 0.0)
+    nsent += send(2, w5("XU", 1024, 1024), "LU", 2048, 1024)
+    loads([("ND0", T.need, 0, O, 0)], came[P["nd"]:P["nd"] + 1])
+    loads([("WT", T.wt, 0, WT1 - B, B), ("KD", T.kid, 0, WT1 - B, B), ("WT", T.wt, WT1 - B, B, WT1), ("KD", T.kid, WT1 - B, B, WT1),
+           ("WT", T.wt, 0, WTW - 2 * B, 2 * B), ("KD", T.kid, 0, WTW - 2 * B, 2 * B)], came[2:])
+    cur[0] = -4
+    for p in range(8, -1, -1):
+        widen(w5("N1", 512 * p), w5("N2", own + 512 * ((p + 2) % 4)), P["n1"][p])
 
     def second():
-        for s, q in enumerate(peers):
-            for p in range(2):
-                bk = xbank()
-                gr = []
+        cur[0] = -2
+        pcs = [(s, q, p) for s, q in enumerate(peers) for p in range(2)]
+        for s, q, p in pcs:
+            y, hi = w5("LH", 1024 * s + 512 * p), w5("HA", 1024 * s + 512 * p)
+            lin("a", hi, y, 2.0 ** -30, 2016.5 * 2.0 ** -30)
+            bk = xbank()
+            mm([(v(bk), [(db(1), y), (db(-2 ** 30), hi)])])
+            lin("x", w5("N2", H * (3 - q) + 512 * p), v(bk), 512.0, 512.0 * 2016)
+        for n, (s, q, p) in enumerate(pcs):
+            y, wt, hi = w5("LU", 2048 * s + 512 * p), w5("HA", 1024 * s + 512 * p), w5("N2", H * (3 - q) + 1024 + 512 * p)
+            x = 512 * n
+            ts(hi, y, M9, M9 + 16384, ALU.add, ALU.subtract)
+            bk = xbank()
+            out = [w5("G2", 256 * (15 - child(q, 2 * p + i)), 256) for i in (0, 1)]
+            widen(w5("X32", x), y, P["wx"][n])
+            if P["route"][n] != "V":
+                mm([(v(bk), [(db(-1), hi), (db(2 ** 41), wt), (df(1), w5("X32", x))])])
                 for i in (0, 1):
-                    hi, y = w5("W2", 256 * (15 - child(q, 2 * p + i)), 256), w5("LH", 1024 * s + 512 * p + 256 * i, 256)
-                    ts(hi, y, 1 / 64, 161 - 31.5 / 64, ALU.mult, ALU.add)
-                    gr.append((w5(bk, 256 * i, 256), [(dh(1), y), (db(-64), hi)]))
-                mm(gr)
-                act(w5("N2", H * (3 - q) + 512 * p), v(bk), 10272.0)
-        for s, q in enumerate(peers):
-            for p in range(2):
-                unpack(2048 * s + 1024 + 512 * p, w5("R2", D * q + 1024 + 512 * p),
-                       [w5("K2", 256 * (15 - child(q, 2 * p + i)), 256) for i in (0, 1)], 0.0)
-        late = [j for j, o in enumerate(ops) if o["kind"] == "x"][-3:]
-        dma(T.ND0[:], T.need[:], 128 * O * 2, [], [("ND0", 0, O)], late)
-        for name, src in (("WT", T.wt), ("KD", T.kid)):
-            dma(v(name, B, 2 * B)[0], src[:], 128 * B * 2, [], [(name, B, 2 * B)], late)
-        for a, b, n in ((3072, 0, H), (1024, 0, H), (0, 1024, 1024)):
-            src = w5("N2", H * (3 - rank) + b, n)
-            dma(w5("N1", a, n)[0], src[0], 256 * n, src[1], w5("N1", a, n)[1], late)
-        for name, src in (("WT", T.wt), ("KD", T.kid)):
-            dma(v(name, 2 * B, WTW)[0], src[:, 0:WTW - 2 * B], 128 * 1728, [], [(name, 2 * B, WTW)], late)
-        if "V" in ROOM_ON:
-            for p in range(4):
-                act(w5("ND1", 512 * p), w5("ND0", 512 * p), 0.0, 256.0)
+                    act(out[i], w5(bk, 256 * i, 256))
+            else:
+                mm([(v(bk), [(db(-1), hi), (db(2 ** 41), wt)])])
+                for i in (0, 1):
+                    tt(out[i], w5("X32", x + 256 * i, 256), w5(bk, 256 * i, 256), ALU.add)
+        cur[0] = -3
+        for p in range(4):
+            widen(w5("R2", D * rank + 512 * p), w5("RM0", 512 * p), P["own"][p])
+        for n, (s, q, p) in enumerate(pcs):
+            y, x = w5("LU", 2048 * s + 1024 + 512 * p), w5("Y32", 512 * (n % 3))
+            lin("r", w5("R2", D * q + 512 * p), y, 2.0 ** -8, -127.5 / 256)
+            widen(x, y, P["wid"][n])
+            ts(w5("R2", D * q + 1024 + 512 * p), x, 255, None, ALU.bitwise_and)
 
     def L(name, c, base=0):
         return v(name, base + c * CW, base + (c + 1) * CW)
 
     def sm(c, k):
-        per = 512 // (8 * CW)
-        a = (c % per) * 8 * CW + k * CW
-        return v("PS%d" % (4 + c // per), a, a + CW)
+        return v("PS%d" % (4 + c), k * CW, (k + 1) * CW)
 
     def kbank(c, i):
         return "PS%d" % (c * (NO // 512) + i)
 
-    def draw(c, wwin, wbias, kwin, nwin, ob, oh):
+    def draw(rd, c, wwin, kwin, nwin, ob, oh):
         o0 = c * NO
+        ga = "GA" if kwin else "GG"
         for i in range(NO // 512):
             a, k0 = o0 + 512 * i, c * CW + 32 * i
-            act(w5("GA", a), ind(wwin, w5(ob, k0, 32)), wbias)
-            tt(w5("GP", a), ind(nwin, w5(oh, k0, 32)), w5("GA", a), ALU.mult)
-        for i in range(NO // 512):
-            act(w5("GK", o0 + 512 * i), ind(kwin, w5(ob, c * CW + 32 * i, 32)))
+            act(w5(ga, a), ind(wwin, w5(ob, k0, 32)), 0.0 if kwin else -2.0 ** -36, 1 / 512 if kwin else 2.0 ** -50)
+            tt(w5("GP", a), ind(nwin, w5(oh, k0, 32)), w5(ga, a), ALU.mult)
+        if kwin:
+            for i in range(NO // 512):
+                widen(w5("GK", o0 + 512 * i), ind(kwin, w5(ob, c * CW + 32 * i, 32)), P["gk"][4 * rd + 2 * c + i])
+        parts = [("GA", db(2 ** 26)), ("GP", db(4096)), ("GK", db(1))] if kwin else [("GG", df(2 ** 50)), ("GP", db(2 ** 36))]
         for i in range(NO // 512):
             bk = kbank(c, i)
-            mm([(v(bk), [(db(1), v("TB"))])], True, False)
-            mm([(w5(bk, 128 * j, 128), [(v("GP", o0 + 4 * i + j, o0 + NO, S), dh(4096)),
-                                        (v("GA", o0 + 4 * i + j, o0 + NO, S), db(2 ** 17))]) for j in range(4)], False, False)
-            mm([(w5(bk, 128 * j, 128), [(v("GK", o0 + 4 * i + j, o0 + NO, S), db(1))]) for j in range(4)], False, True)
-            scan(w5("SC", c * SW + 512 * i), v("DL"), v(bk), ALU.add, ALU.max)
-        act(w5("QB", c * QW + 16, 128), ind(w5("SC", c * SW, SW), v("OQ")), KBIAS)
+            for n, (nm, k) in enumerate(parts):
+                for js in ([[0, 1, 2, 3]] if nm != "GG" else P["split"]):
+                    mm([(w5(bk, 128 * j, 128), [(v(nm, o0 + 4 * i + j, o0 + NO, S), k)]) for j in js],
+                       n == 0 and js[0] == 0, n == len(parts) - 1, [(bk, 0, 512)])
+            scan(w5("SC", o0 + 512 * i), v("DL"), v(bk), ALU.add, ALU.max)
+        ts(w5("QI", 72 * c, 64), v("SC", o0 + 15, o0 + NO, 16), 4095, None, ALU.bitwise_and)
+        lin("Q", w5("QB", c * QW + 16, 128), ind(w5("QI", 72 * c, 72), v("OQ")), 1.0, -2048.0)
         mm([(sm(c, 0), [(w5("QB", c * QW + 16 - S * k, 128), w5("EE", k * CW, CW)) for k in range(NSH)])])
-        ts(L("HH", c), sm(c, 0), M12, M12, ALU.add, ALU.subtract)
-        tt(L("QC", c), sm(c, 0), L("HH", c), ALU.subtract)
+        lin("e", L("QC", c), sm(c, 0), 1.0, 0.0)
+        return sm(c, 0) if P["ps"] else L("QC", c)
 
-    CD = 32760 + 4097 * 160 + 15 - 477 * 2048
+    def goes(rd, c):
+        mm([(sm(c, 3), [(db(1), L("CP", c)), (db(-4), L("UP", c))] + ([(db(8), L("BO", c))] if rd == 2 else []))])
+        a = 4 * CW * c
+        for k in range(4):
+            ts(w5("MK", a + CW * k, CW), sm(c, 3), float(k - 480), None, ALU.is_equal)
+        if c == 0:
+            scan(w5("IK", 0, 4 * CW), w5("RS", 0, 4 * CW), w5("MK", 0, 4 * CW), ALU.mult, ALU.add)
+        else:
+            for k in range(4):
+                b = a + CW * k
+                scan(w5("IK", b, CW), w5("RS", 4 * CW, CW), w5("MK", b, CW), ALU.mult, ALU.add, w5("IK", b - 3 * CW - 1, 1))
+        mm([(w5("PS6", a, 4 * CW), [(v("BLK"), w5("IK", a, 4 * CW)), (v("UT"), w5("MK", a, 4 * CW))])])
+        act(w5("SG", a, 4 * CW), w5("PS6", a, 4 * CW), CAP + 0.5 - 4096, -1.0, AF.Sign)
+        mm([(sm(c, 3), [(db(1), w5("SG", a + CW * k, CW)) for k in range(4)])])
+        act(L("GS", c), sm(c, 3))
+
+    CD = 32768 + 2 * 327680 + 160 - 1310720 + 15 + 3 * 2048
     for rd in range(RO):
         for c in range(NC):
             cur[0] = c
             if rd == 0:
-                draw(c, v("WT", 0, B), 0.0, v("KD", 0, B), w5("N2", H * (3 - rank), H), "OB", "OH")
+                q = draw(rd, c, v("WT", 0, B), v("KD", 0, B), w5("N2", own, H), "OB", "OH")
             else:
-                w = 6576 if rd == 1 else WTW
-                draw(c, v("WT", 0, w), 0.0, v("KD", 0, w), v("N1"), "OB", "OH")
-            ts(L("OB2", c), L("QC", c), 2047.5, None, ALU.add)
-            act(L("CP", c), L("QC", c), 167.5, 1 / 256)
-            act(L("UP", c), L("QC", c), 161.5, 1 / 1024)
-            base = [(df(592), L("QC", c)), (dh(1), L("BS", c))]
+                w = WT1 if rd == 1 else WTW
+                q = draw(rd, c, v("WT", 0, w), v("KD", 0, w), v("N1"), "OB", "OH")
+            lin("o", L("OB2", c), q, 1.0, 2048.0)
+            lin("p", L("CP", c), q, 1 / 256, 167.5 + 1 / 512)
+            lin("u", L("UP", c), q, 1 / 1024, 161.5 + 1 / 2048)
+            base = [(db(1), L("BS", c))] + ([(dh(611), L("TT", c, 128 * (rd - 1)))] if rd else []) + [(dh(592), L("QC", c))]
+            mm([(sm(c, 1), base + [(db(-37), L("CP", c))])])
+            lin("h", L("H2", c), sm(c, 1), 2.0 ** -35, 0.0)
+            mm([(sm(c, 2), base + [(dh(2011), L("CP", c)), (db(-8192), L("UP", c)), (db(-2 ** 35), L("H2", c))])])
+            lin("H", L("OH2", c), sm(c, 2), 1.0, 1023.5 + 983040)
             if rd:
-                base.append((dh(611), L("TT", c, 128 * (rd - 1))))
-            mm([(sm(c, 1), base + [(db(-37), L("CP", c))]),
-                (sm(c, 2), base + [(dh(2011), L("CP", c)), (db(-8192), L("UP", c))])])
-            ts(L("H2", c), sm(c, 1), M11, M11, ALU.add, ALU.subtract)
-            tt(L("T2", c), sm(c, 2), L("H2", c), ALU.subtract)
-            ts(L("OH2", c), L("T2", c), 1023.5 + 983040, None, ALU.add)
-            mm([(sm(c, 3), [(db(1), L("CP", c)), (db(-4), L("UP", c))] + ([(db(8), L("BO", c))] if rd == 2 else []))])
-            a = 4 * CW * c
-            for k in range(4):
-                ts(w5("MK", a + CW * k, CW), sm(c, 3), float(k - 480), None, ALU.is_equal)
-            if c == 0:
-                scan(w5("IK", 0, 4 * CW), w5("RS", 0, 4 * CW), w5("MK", 0, 4 * CW), ALU.mult, ALU.add)
-            else:
-                for k in range(4):
-                    b = a + CW * k
-                    scan(w5("IK", b, CW), w5("RS", 4 * CW, CW), w5("MK", b, CW), ALU.mult, ALU.add, w5("IK", b - 3 * CW - 1, 1))
-            mm([(w5("PS6", a, 4 * CW), [(v("BLK"), w5("IK", a, 4 * CW)), (v("UT"), w5("MK", a, 4 * CW))])])
-            act(w5("SG", a, 4 * CW), w5("PS6", a, 4 * CW), CAP + 0.5 - 4096, -1.0, AF.Sign)
-            mm([(L("PS7", c), [(db(1), w5("SG", a + CW * k, CW)) for k in range(4)])])
-            act(L("GS", c), L("PS7", c))
+                goes(rd, c)
         if rd == 0:
-            cur[0] = -2
             second()
+            for c in range(NC):
+                cur[0] = c
+                goes(rd, c)
         for c in range(NC):
             cur[0] = c
             o0 = c * NO
-            draw(c, v("W2"), -129.0, v("K2"), v("N2"), "OB2", "OH2")
-            act(L("CP2", c), L("QC", c), 167.5, 1 / 256)
-            mm([(sm(c, 4), [(df(16), L("QC", c)), (db(-2048), L("CP", c)), (db(8192), L("UP", c)),
-                            (db(-4096), L("CP2", c)), (db(-1), L("CP2", c))])])
-            ts(L("OR", c), sm(c, 4), float(CD), None, ALU.add)
+            q = draw(rd, c, v("G2"), None, v("N2"), "OB2", "OH2")
+            lin("P", L("CP2", c), q, 1 / 256, 167.5 + 1 / 512)
+            lin("c", L("CQ", c), q, 1 / 128, 175.5 + 1 / 256)
+            mm([(sm(c, 4), [(db(-2048), L("CP", c)), (db(8192), L("UP", c)), (dh(16), L("QC", c)),
+                            (db(-1), L("CP2", c)), (db(-2048), L("CQ", c))])])
+            lin("d", L("OR", c), sm(c, 4), 1.0, CD)
             act(L("DV", c), sm(c, 4), CD + 1)
             for i in range(NO // 512):
                 a = o0 + 512 * i
                 gi = ind(v("R2"), w5("OR", c * CW + 32 * i, 32))
-                if ROOM_ON[(rd * NC + c) * 2 + i] == "A":
-                    act(w5("GR", a), gi)
-                    mm([(v(kbank(c, i)), [(db(256), w5("ND0", a)), (db(-1), w5("GR", a))])])
+                if P["room"][(rd * NC + c) * 2 + i] == "A":
+                    act(w5("GK", a), gi)
+                    mm([(v(kbank(c, i)), [(db(1), w5("ND0", a)), (db(-1), w5("GK", a))])])
                     act(w5("VI", a), v(kbank(c, i)), 0.0, 1.0, AF.Relu)
                 else:
-                    tt(w5("VI", a), gi, w5("ND1", a), ALU.is_lt)
+                    tt(w5("VI", a), gi, w5("ND0", a), ALU.is_lt)
             terms = [(db(-1), L("GS", c))]
             if rd:
                 tt(L("EQ", c), L("DV", c), L("KV", c) if rd == 1 else L("S12", c), ALU.is_equal)
@@ -435,15 +431,18 @@ def build(g, T, topo, rank):
             terms += [(w5("SEL", 15 - r, 128), v("VI", o0 + r, o0 + NO, 16)) for r in range(16)]
             mm([(sm(c, 5), terms)])
             kp = L("KP", c, 128 * rd)
-            ts(kp, sm(c, 5), 2.5, None, ALU.is_le)
+            if "k" in P["act"]:
+                act(kp, sm(c, 5), 3.0, -1.0, AF.Relu)
+            else:
+                ts(kp, sm(c, 5), 2.5, None, ALU.is_le)
             if rd < 2:
                 up = ([L("TT", c)] if rd else []) + [L("GS", c)]
-                mm([(sm(c, 6), [(dh(1), L("BB", c))] + [(dh(1237), x) for x in up] + [(dh(-1237), kp)]),
-                    (sm(c, 7), [(dh(1), L("BA", c))] + [(dh(-724), x) for x in up] + [(dh(724), kp)])])
-                ts(L("OB", c), sm(c, 6), 2048.0 + 4 * 1237, None, ALU.add)
-                ts(L("OH", c), sm(c, 7), 1024.0 - 4 * 724 + 3072, None, ALU.add)
-                mm([(L("PS7", c, 128), [(db(1), x) for x in up] + [(db(-1), kp)])])
-                act(L("TT", c, 128 * rd), L("PS7", c, 128), 4.0)
+                mm([(sm(c, 6), [(db(1), L("BB", c))] + [(dh(1237), x) for x in up] + [(dh(-1237), kp)]),
+                    (sm(c, 7), [(db(1), L("BA", c))] + [(dh(-724), x) for x in up] + [(dh(724), kp)])])
+                lin("b", L("OB", c), sm(c, 6), 1.0, 2048.0 + 4 * 1237)
+                lin("n", L("OH", c), sm(c, 7), 1.0, 1024.0 - 4 * 724 + 3072)
+                mm([(sm(c, 1), [(db(1), x) for x in up] + [(db(-1), kp)])])
+                act(L("TT", c, 128 * rd), sm(c, 1), 4.0)
                 tt(L("KV", c, 128 * rd), kp, L("DV", c), ALU.mult)
             if rd == 1:
                 tt(L("BO", c), L("KP", c), kp, ALU.mult)
@@ -452,7 +451,7 @@ def build(g, T, topo, rank):
                 tt(L("U2", c), L("S12", c), L("U1", c), ALU.subtract)
                 act(L("B12", c), L("U1", c), -1.0)
                 act(L("A12", c), L("U2", c), -1.0)
-                ts(L("NN", c), L("S12", c), 0.0, None, ALU.is_equal)
+                act(L("NN", c), L("S12", c), 1.0, -1.0, AF.Relu)
             if rd == 2:
                 for y, dst, dv, old, tmp in (("YA", T.ya, "DA", "A12", "U1"), ("YB", T.yb, "DBB", "B12", "U2")):
                     tt(L(tmp, c), kp, L(dv, c), ALU.mult)
@@ -461,101 +460,18 @@ def build(g, T, topo, rank):
     return ops, nsent
 
 
-def plan(ops, succ, prio):
-    n = len(ops)
-    left = [len(o["deps"]) + len(o.get("after", [])) for o in ops]
-    ready = [i for i in range(n) if left[i] == 0]
-    fin, dep, free, pipe, last, order, more = [0.0] * n, [0.0] * n, {}, 0.0, {}, [], {}
-    while ready:
-        st = {}
-        for i in ready:
-            o = ops[i]
-            t = max(free.get(o["q"], 0.0), dep[i])
-            for b in o["banks"]:
-                for q, j in last.get(b, {}).items():
-                    if q != o["q"]:
-                        t = max(t, fin[j] + LAT_X)
-            st[i] = t
-        i0 = min(ready, key=st.get)
-        i = max([k for k in ready if ops[k]["q"] == ops[i0]["q"] and st[k] <= st[i0] + SLACK], key=lambda k: prio[k])
-        o = ops[i]
-        for b in o["banks"]:
-            for q, j in last.get(b, {}).items():
-                if q != o["q"]:
-                    more.setdefault(i, set()).add(j)
-            last.setdefault(b, {})[o["q"]] = i
-        if o["kind"] in "dr":
-            free[o["q"]] = st[i] + (0.1 if o["kind"] == "d" else 1.0)
-            pipe = max(pipe, st[i] + 1.5) + o["dur"]
-            fin[i] = pipe
-        elif o["kind"] == "x":
-            fin[i] = st[i] + o["dur"]
-        else:
-            fin[i] = free[o["q"]] = st[i] + o["dur"]
-        order.append(i)
-        ready.remove(i)
-        for j in succ[i]:
-            left[j] -= 1
-            if i in ops[j]["deps"]:
-                dep[j] = max(dep[j], fin[i] + (LAT_S if ops[j]["q"] == o["q"] else LAT_X))
-            if left[j] == 0:
-                ready.append(j)
-    return max(fin), order, more
-
-
-def replay(ops, order, more, m):
-    fin, free, pipe = [0.0] * len(ops), {}, 0.0
+def schedule(ops):
+    al = "0123456789abcdefghijklmnopqrstuvwxyzABCDEFGHIJKLMNOPQRSTUVWXYZ"
+    order = [al.index(ORDER[k]) * 62 + al.index(ORDER[k + 1]) for k in range(0, len(ORDER), 2)]
+    assert sorted(order) == list(range(len(ops)))
+    last, done = {}, set()
     for i in order:
         o = ops[i]
-        t = free.get(o["q"], 0.0)
-        for d in o["deps"]:
-            t = max(t, fin[d] + m[3])
-        for d in more.get(i, ()):
-            t = max(t, fin[d] + m[3])
-        if o["kind"] in "dr":
-            free[o["q"]] = t + (0.1 if o["kind"] == "d" else 1.0)
-            pipe = fin[i] = max(pipe, t + 1.5) + o["dur"] * m[4 if o["kind"] == "d" else 5]
-        elif o["kind"] == "x":
-            fin[i] = t + o["dur"]
-        else:
-            fin[i] = free[o["q"]] = t + o["dur"] * m[2 if o["q"] == "P" else o["g"]]
-    return max(fin)
-
-
-CASES = [(0.92, 0.92, 1.05, 0.1, 0.83, 0.83), (0.92, 0.92, 0.85, 0.15, 0.83, 1.6), (1.27, 1.6, 1.1, 0.06, 0.83, 0.83),
-         (1.36, 1.05, 1.3, 0.12, 1.2, 1.2)]
-SEED, HEAT = 1, 0.0
-CACHE = {}
-
-
-def schedule(ops):
-    n = len(ops)
-    succ = [[] for _ in ops]
-    for i, o in enumerate(ops):
-        for d in list(o["deps"]) + o.get("after", []):
-            succ[d].append(i)
-    if "prio" not in CACHE:
-        prio = [0.0] * n
-        for i in range(n - 1, -1, -1):
-            prio[i] = ops[i]["dur"] + (1.5 if ops[i]["kind"] in "dr" else LAT_X) + max([prio[j] for j in succ[i]] + [0.0])
-        prio = np.array([p + {-1: PRE, -2: PRE2}.get(o["c"], -SKEW * o["c"]) for p, o in zip(prio, ops)])
-        rng = np.random.default_rng(SEED)
-        base = None
-        for it in range(TUNE + 1):
-            p = prio.copy()
-            if it:
-                a, w = int(rng.integers(0, n)), int(rng.integers(1, 30))
-                p[a:a + w] += SIGMA * rng.normal() + 0.5 * SIGMA * rng.normal(size=len(p[a:a + w]))
-            _, order, more = plan(ops, succ, p)
-            t = np.array([replay(ops, order, more, m) for m in CASES])
-            if base is None:
-                base, best = t, 1.0
-            if (t / base).mean() <= best + HEAT * (1 - it / TUNE) * rng.random():
-                best, prio = (t / base).mean(), p
-        CACHE["prio"] = prio
-    _, order, more = plan(ops, succ, CACHE["prio"])
-    for i, m in more.items():
-        ops[i]["deps"] |= m
+        assert o["deps"] <= done
+        done.add(i)
+        for b in o["banks"]:
+            o["deps"] |= set(j for q, j in last.get(b, {}).items() if q != o["q"])
+            last.setdefault(b, {})[o["q"]] = i
     return order
 
 

@@ -3,40 +3,36 @@ from concourse.mybir import AluOpType as ALU, ActivationFunctionType as AF
 
 NR, B, H, D, O, CAP, RO = 4, 4096, 2048, 2048, 2048, 512, 3
 NC = 2
-S = 16 // NC
-NSH = 16 // S
 CW = 128 // NC
 NO = O // NC
 QW = 144
-P = {"route": "VVVVVV",
-     "wx": "AAAAAA", "wid": "GGGGGG", "own": "GGGG", "n1": "GGGGGGGGGG",
-     "gk": "AAAAAAAAAAAA", "room": "VVVVVVVVVVVV",
-     "act": "xyzrdbnkQpP",
-     "banks": "767676012301", "split": [[0, 1], [2, 3]], "rm": 1, "nd": 1, "ps": 0}
+P = {"room": "VVVVVVVVVAVA", "gate": "V", "banks": "767676012301", "act": "xyzrdbnkQoup", "rm": 1, "nd": 1}
 M9 = 1.5 * 2.0 ** 32
-WTW, WT1 = 9056, 6576
-DB = [1, -1, 64, 512, 256, 2 ** 17, 4096, 2 ** 26, 2 ** 36, 2 ** 41, -2 ** 30, -37, -4, 8,
-      -2048, 8192, -8192, -4096, -2 ** 35]
-DH = [1237, -1237, -724, 724, 611, 2011, 592, 16]
+WTW, WT1, HX = 9056, 6576, 2608
+DB = [1, -1, 64, 512, 256, 2 ** 17, 4096, 2 ** 26, 2 ** 36, 2 ** 41, -2 ** 30, -37, 8,
+      -2048, 2608, -10432, -4096, -6144, 8192]
+DH = [1237, -1237, -724, 724]
+DS = [1, -4, 611]
 DF = [1, 2 ** 50]
 
 BF, F16, F32, I32, U16 = "bfloat16", "float16", "float32", "int32", "uint16"
 SB = {
     "WT": (WTW, BF), "KD": (WTW, BF), "N1": (5120, BF), "NR0": (H, BF), "RM0": (D, BF), "ND0": (O, BF),
-    "G2": (B, F32), "N2": (NR * H, BF), "R2": (NR * D, I32), "XU": (2048, U16), "XH": (1024, F16),
-    "LU": (6144, U16), "LH": (3072, F16), "HA": (3072, F16), "X32": (3072, F32), "Y32": (1536, I32),
+    "G2": (B, F32), "N2": (NR * HX, BF), "R2": (NR * D, I32), "XU": (2048, U16), "XH": (1024, F16),
+    "LU": (6144, U16), "LH": (3072, F16), "HA": (3072, F16), "X32": (2048, F32), "Y32": (1536, I32),
     "GA": (O, BF), "GK": (O, BF), "GG": (O, F32), "GP": (O, F16), "VI": (O, BF),
-    "SC": (O, I32), "QI": (NC * 72, I32), "QB": (NC * QW, F16),
+    "SC": (O, I32), "QI": (4 * 72, I32), "QB": (4 * QW, F16),
     "BEG": (128, I32), "SAL": (128, I32), "I1": (128, I32), "I2": (128, I32), "I3": (128, I32), "I4": (128, I32),
-    "F1": (128, F32), "BB": (128, F16), "BA": (128, F16), "BS": (128, F16),
+    "F1": (128, F32), "BB": (128, F16), "BA": (128, F16), "BS": (128, F16), "BY": (128, F16), "CC": (128, F16),
     "OB": (128, U16), "OH": (128, U16), "OB2": (128, U16), "OH2": (128, U16), "OR": (128, U16), "OQ": (8, U16),
-    "QC": (128, F16), "H2": (128, F16),
-    "CP": (128, BF), "UP": (128, BF), "CP2": (128, BF), "CQ": (128, BF), "MK": (512, BF), "IK": (512, BF), "SG": (512, BF),
+    "H2": (128, I32), "H3": (128, I32),
+    "CP": (128, BF), "UP": (128, BF), "MK": (512, BF), "IK": (512, BF), "SG": (512, BF),
     "RS": (512, BF), "DL": (512, BF), "GS": (128, BF), "TT": (256, BF), "KP": (384, BF),
-    "EQ": (128, BF), "BO": (128, BF),
+    "EQ": (128, BF), "BO": (128, BF), "NN": (128, BF), "NM": (128, BF),
     "DV": (128, F32), "KV": (256, F32), "S12": (128, F32), "B12": (128, F32), "A12": (128, F32), "U1": (128, F32),
-    "U2": (128, F32), "NN": (128, F32), "DA": (128, F32), "DBB": (128, F32), "YA": (128, F32), "YB": (128, F32),
-    "ONE": (144, F32), "EE": (NSH * CW, BF), "PI": (2, I32), "PJ": (2, I32), "PF": (2, F32),
+    "U2": (128, F32), "DA": (128, F32), "DBB": (128, F32), "YA": (128, F32), "YB": (128, F32),
+    "ONE": (144, F32), "EE": (128, BF), "E5": (128, F16), "E6": (128, BF),
+    "PI": (2, I32), "PJ": (4, I32), "PF": (8, F32), "SH": (256, BF), "MS": (128 * 12, F16),
     "JF": (144, F32), "MF": (128, F32), "OF": (8, F32), "OG": (8, F32),
     "SEL": (144, BF), "BLK": (128, BF), "UT0": (128, BF), "UT": (128, BF),
     "MB": (128 * len(DB), BF), "MH": (128 * len(DH), F16), "MFF": (128 * len(DF), F32),
@@ -47,13 +43,15 @@ for _i in range(8):
 SEMAPHORES = ["cV", "cA", "cP", "cG", "sent"] + ["dm%d" % i for i in range(24)] + ["ar%d" % i for i in range(12)]
 
 CY, PCY, GF, RATE = 0.83e-3 * 1.1, 0.0005 * 1.1, 1.56, 250e3
-ORDER = "00050B01060P0203040Q0D070I0z0y0A0a0F0b0e080c0d0H0g0p0j0G0m0L0h0i0V0U0M090n0f0C0R0T170w0v160E0K0X0W0Y131O1R0N1Q1M110Z1012140S0o150l0x0J0q0t0O0s181a0r1b1W191U1X1V0u2l1c2m2024211i2j1Z1Y1j0k2k1g1h1p1N1S1L1T1k1o1f1d1e2I2O2U2L2X2p1q1t2t25222q2u2627231y1w281r2n2o1x291v1u1z2v2r2J2a2M2K1l1m1n3x1A3v1P3u3w2R2w2s2b1s3l31362d2N3g3b1E302e2c353p3a3f3k2P323q2Q34333738393c3h3m2f3r2S3i3j2V3e3n3d2x3o1B1C1D2y2T2g3z3C1F1G1H1J1I1K3t3s3Q2h3A3U3R3S3T3F3I4f4d2W2z2Y2Z2A2i3B2C4h4l4m2E4i2B4I3y3E2D3V3D3G3O4e4g4n4K3H3J2F3P4j3W2G4o4k3L3K2H4p4L4q3N4M4Q3X4r4R4s4J4u3M4t4S4v404w4N4O3Y3Z4x4T4y4z4P414U4442434A4V4B4W45484X4Z46474H4Y4F4C50494D4E515d4a54534b5i4c555f5e5g565h4G5j5n5758595M5k5l5o5p5m5N5q5r5a5O5R5P5S5W5b525s5Q5t5u5w5c5v6o6q5x5X5T5y5U5z5Y5A5C5V5Z5B60616p6r6s6w626x6t6365676u645E5G665D5F6873715H6v6y695I756z6a6b6A6B6C79746D6e6F6E6G5J6I6H7a726L6J6K7b765K775L7c786M6N6c7d6d6T6i6U6V6f6h6j6g6O7e6P6Q7G7f6k7g6W7h7i7H7j6R6l7k7l6m7E7J6n7n7o7m7I7O7K7p7q707F6X6S7w7z7y7A7P7r7Q7L7s7t8d8f7M7u7R7x7N8e7S8g8i7T8h8n8j7U7V7W7X8P8R7C7v8o8p7Z8k8l7Y8q8081838m8T828r868Q8s6Z7B6Y7D8t8u8w8U8X8y8S8v8x87848z8V9n9p8C8A8Y8Z9r9v9s858W8B8F8E888D9o9q90918G9t929w939x8K9u948H8I969y95978998998J9z9b9d9A9B9C9c9E9a8a8b9D8c9F9G9H8L8M8N8O9f9g9I9K9J9N9O9e9h9k9L9i9M9l9S9P9T9Q9j9m9U9R"
+ENGINE = "AAAAAAAAAAVAVAAAAAVAVAAVGVVVAVAGAAAVAVAAGAGGGGGVVAVAVVVVAAVAVAVVAVAAAAAVAVAAVAVGVAVAVAVGGGGGGGGAGAAAAAGAGAGAAAAAVVAAAAVAAAAVVAAAAVVVAAVAAAAAAAAAAAAAAVAAAAAVVVAAVAAAVVVAAAVAVVAVAAVAVVAAAAAAAAAAAAVAVVAVVAAVVVVVAAVA"
+ORDER = "00050y01060203040B0z0A0C0D070G0d0a0u0K0Y0E1b0m0j0F0N090b0e0p0c0J0Z0v0h080H0L160I1d0X110O0P1o1p1f0g1j0t1l1e240w181g12170r0n14293Q26130o0S1m1n250l0M1a0k1c1h1k1q1s151i190i0R0V1r2g2h2H1t2i2F0Q0T0U2I2m2P282q1A1I2Q1y1L1B2K1u272a1w1v1x1H2b2l2j0x2r2k1K2J2R2G0q1z1N2S2n2o2e2s231C1G3U2L2c2M2N1O2f2p0s2t1Q1J3d0f1P2O2u0W2d1M2T371R3g2U102v343j1S1E3X3x1D38392w2x2W2z2Y3a2V3e353s1F1W3n363C3r3B3m3t3o3b3f3c2B3L3w2X3G3D3y3h3v3p3q3u3M303H3N3I3k1T1U1V1X1Y1Z2120223i42453R3V3l3E3F2Z2C2A3z3A2y313O3P3J3K324g4h2D3S3Z4r4t4X4Z4d3Y4a47443T43464j2E4l40334k4i4s4e4u4b4v4y544z4w5141483W4Y504f4c4A4x4m524D4B535556494C4E4n4F4G4o4L4M4I4J57594N4K4p585a4H5b4q5c4O5h5e5f5i5d5j5g4P4Q4V5k4R4S5v4T5l5D5m5t5n4U5x5y5w5u5U5z5o5E5F5S5V5X5A5p5B6263645Y5G5C5H5W5T5I5r5q5J5K5Z5L5O5P6s655M6u5N6061665Q6h6w5s5R674W6v6t686z6d6e6A696a7a6x6b6f6i7c6B6c6y6g6k6l6E6C7b6m6j7d6n6D6F7e7h6G7f7i6o6H6I6M6p6J6K6N6q7g7j6P7k7m7n6O7l7o6L6r7p7q6Q7u7v7r7s6R6X6S7w7x7t7y6T6U6Y7W7S7U7z6Z7T7V7F707G6V7Y7X7D7A7Z80827B7C7181728384858j8h867H738r7I7J8k6W878m8n88898s8l7E8b8t8i8a8e8d8u8c7K8T7L8o8p8f8G8R8q8g7M8v8Y8U8w748x8y8S7Q7O768C8D8Z8A8E8H8z789v9t797R8V8W8B908J758L8I8F8K9w8X7N9391777P9A9x9B9492959u8M9C9y9z96979F9D98999b9G9E8N9c9H8O9h8P9a9e9J9I9d8Q9N9O9K9L9T9U9Q9M9P9R9f9i9g9S9j9k9V9l9p9W9q9m9Xa1a29r9Y9n9Za39s9oa0a4"
 
 
 def build(g, T, topo, rank):
     ops = []
     acc = {}
     cur = [-1]
+    dry = []
 
     def v(name, a=0, b=None, step=1):
         if b is None:
@@ -65,6 +63,9 @@ def build(g, T, topo, rank):
         return (win[0].indirect(off[0]), win[1] + off[1], 16 * off[2], win[3], True)
 
     def add(q, fn, dur, reads, writes, kind="c", extra=()):
+        if dry:
+            dry[-1].append((q, fn, dur, reads, writes))
+            return None
         i = len(ops)
         deps = set(extra)
         for (n, a, b) in reads:
@@ -113,19 +114,38 @@ def build(g, T, topo, rank):
     def ms(out, c):
         return add("V", lambda: g.vector.memset(out[0], c), vcost(out, [out]), [], out[1])
 
-    def scan(out, d0, d1, op0, op1, init=None):
-        i0, r = (init[0], init[1]) if init else (0.0, [])
-        return add("V", lambda: g.vector.tensor_tensor_scan(out[0], d0[0], d1[0], i0, op0, op1),
-                   vcost(out, [d0, d1]), d0[1] + d1[1] + r, out[1])
+    def scan(out, d0, d1, op0, op1):
+        return add("V", lambda: g.vector.tensor_tensor_scan(out[0], d0[0], d1[0], 0.0, op0, op1),
+                   vcost(out, [d0, d1]), d0[1] + d1[1], out[1])
 
     def act(out, in0, bias=0.0, scale=1.0, func=AF.Identity):
         d = 0.065 + out[2] * GF * CY if len(in0) == 5 else max(64, out[2]) * CY + 0.03
         return add("A", lambda: g.scalar.activation(out[0], in0[0], func, bias=float(bias), scale=float(scale)), d, in0[1], out[1])
 
+    npick = [0]
+
+    def pick(on, ways):
+        npick[0] += 1
+        on = ENGINE[npick[0] - 1] if ENGINE else on
+        rec = {}
+        for k, fs in ways.items():
+            rec[k] = []
+            for f in fs if isinstance(fs, list) else [fs]:
+                dry.append([("X", None, 0.0, [], [])])
+                if f:
+                    f()
+                rec[k].append(dry.pop()[-1])
+        for n, (q, fn, dur, _, _) in enumerate(rec[on]):
+            i = add(q, fn, dur, sum((r[n][3] for r in rec.values()), []), sum((r[n][4] for r in rec.values()), []), "c" if fn else "n")
+            ops[i]["alt"] = {k: (r[n][0], r[n][2], set(x[0] for x in r[n][3] + r[n][4] if x[0].startswith("PS")),
+                                 int(any(x[0][0] == "O" and x[0][1] in "BHRQ" for x in r[n][3]))) for k, r in rec.items()}
+            ops[i]["grp"], ops[i]["on"] = npick[0] - 1, on
+            ops[i]["banks"], ops[i]["g"] = ops[i]["alt"][on][2:]
+        return i
+
     def lin(tag, out, in0, scale, bias):
-        if tag in P["act"]:
-            return act(out, in0, bias, scale)
-        return ts(out, in0, float(scale), float(bias), ALU.mult, ALU.add)
+        return pick("A" if tag in P["act"] else "V", {"A": lambda: act(out, in0, bias, scale),
+                    "V": lambda: ts(out, in0, float(scale), float(bias), ALU.mult, ALU.add)})
 
     def mm(groups, first=None, end=None, more=()):
         r, w, d = [], list(more), 0.03
@@ -152,7 +172,10 @@ def build(g, T, topo, rank):
         return add("G", lambda: g.affine_select(out[0], in0[0], pat, op, 0.0, base, mult), 0.17 + 2 * out[2] * CY, in0[1], out[1])
 
     def widen(out, in0, on="G"):
-        return asel(out, in0, [[0, out[2]]], ALU.is_ge, 0, 0) if on == "G" else act(out, in0) if on == "A" else cp(out, in0)
+        ways = {"A": lambda: act(out, in0), "V": lambda: cp(out, in0)}
+        if len(in0) == 4:
+            ways["G"] = lambda: asel(out, in0, [[0, out[2]]], ALU.is_ge, 0, 0)
+        return pick(on, ways)
 
     nd = [0]
 
@@ -189,16 +212,31 @@ def build(g, T, topo, rank):
     for n, c in enumerate(DB[1:]):
         lin("x" if n % 3 == 2 else "-", db(c), db(1), c, 0.0)
     for c in DH:
-        ts(dh(c), db(1), float(c), None, ALU.mult)
+        lin("-", dh(c), db(1), c, 0.0)
     for c in DF[1:]:
         act(df(c), df(1), 0.0, c)
-    for k in range(NSH):
-        asel(v("EE", k * CW, (k + 1) * CW), v("ONE", 0, CW), [[-NSH, CW]], ALU.is_equal, -k, 1)
+    asel(v("EE"), v("ONE", 0, 128), [[-1, 2], [-2, 2], [-4, 32]], ALU.is_equal, 0, 1)
+    lin("-", v("E5"), v("EE"), 592.0, 0.0)
+    lin("-", v("E6"), v("EE"), 16.0, 0.0)
     iota(v("PI", 0, 1), [[0, 1]], 0, 1)
     ts(v("PJ", 0, 1), v("PI", 0, 1), 112, None, ALU.bitwise_and)
-    ts(v("PJ", 1, 2), v("PI", 0, 1), 15, None, ALU.bitwise_and)
-    cp(v("PF", 0, 1), v("PJ", 0, 1))
-    ts(v("PF", 1, 2), v("PJ", 1, 2), 8.0, None, ALU.mult)
+    for n, m in enumerate((3, 4, 8)):
+        ts(v("PJ", n + 1, n + 2), v("PI", 0, 1), m, None, ALU.bitwise_and)
+    cp(v("PF", 0, 4), v("PJ"))
+    ts(v("PF", 4, 5), v("PF", 3, 4), 0.125, None, ALU.mult)
+    ts(v("PF", 5, 6), v("PF", 4, 5), -1.0, 1.0, ALU.mult, ALU.add)
+    ts(v("PF", 6, 7), v("PF", 2, 3), 8.0, v("PF", 1, 2)[0], ALU.mult, ALU.add)
+    ops[-1]["deps"].add(len(ops) - 4)
+    ts(v("PF", 7, 8), v("PF", 6, 7), v("PF", 3, 4), 8.0, ALU.add, ALU.mult)
+    ts(v("PF", 1, 2), v("PF", 3, 4), -4.0, v("PF", 7, 8)[0], ALU.mult, ALU.add)
+    ops[-1]["deps"].add(len(ops) - 2)
+    asel(v("SH", 0, 128), v("ONE", 0, 128), [[-1, 128]], ALU.is_equal, 8, 1)
+    asel(v("SH", 128, 256), v("ONE", 0, 128), [[-1, 128]], ALU.is_equal, -8, 1)
+    for n, k in enumerate(DS):
+        for b in (0, 1):
+            for a in (0, 1):
+                ts(w5("MS", 128 * (4 * n + 2 * b + a), 128), db(1) if a == b else w5("SH", 128 * b, 128), v("PF", 5 - b, 6 - b),
+                   float(k), ALU.mult, ALU.mult)
     iota(v("JF"), [[1, 144]], -15, 0)
     iota(v("MF"), [[16, 8], [0, 16]], 0, 0)
     iota(v("OF"), [[1, 8]], 0, 0)
@@ -211,10 +249,11 @@ def build(g, T, topo, rank):
     ms(v("DL"), 256.0)
     ms(v("DL", 0, 512, 16), -2.0 ** 24)
     ms(v("RS"), 1.0)
-    ms(v("RS", 0, 3 * CW + 1, CW), 0.0)
+    ms(v("RS", 0, 512, 128), 0.0)
     ms(v("QB"), 0.0)
-    for c in range(NC):
-        ms(v("QI", 72 * c + 64, 72 * c + 72), 2048)
+    ms(v("CC", 0, 64), 555.0 + 37 * 160 - 2 * HX)
+    ms(v("CC", 64, 128), 482.0)
+    ms(v("QI"), 2048)
 
     widen(v("OB"), v("BEG"), "A")
     act(v("F1"), v("BEG"), 0.0, 37.0)
@@ -223,7 +262,7 @@ def build(g, T, topo, rank):
     cp(v("OH"), v("I2"))
     act(v("BB"), v("BEG"), -2048.0)
     act(v("BA"), v("I2"), -1024.0)
-    act(v("I3"), v("SAL"), 331.0)
+    act(v("I3"), v("SAL"), 0.0)
     ts(v("I4"), v("I3"), H - 1, None, ALU.bitwise_and)
     act(v("BS"), v("I4"), -1023.5)
 
@@ -263,9 +302,9 @@ def build(g, T, topo, rank):
     def mine(name, i):
         return v(name, child(rank, i), B, 16)
 
-    own = H * (3 - rank)
+    own = HX * (3 - rank)
     for p in range(2):
-        ts(w5("N2", own + 1024 * p, 1024), w5("NR0", 1024 * p, 1024), -32.0, 512.0, ALU.add, ALU.mult)
+        lin("-", w5("N2", own + 1024 * p, 1024), w5("NR0", 1024 * p, 1024), 512.0, -16384.0)
     for p in range(2):
         bk = "PS%d" % (4 + p)
         mm([(w5(bk, 256 * i, 256), [(db(64), mine("WT", 2 * p + i)), (db(1), w5("NR0", 512 * p + 256 * i, 256))]) for i in (0, 1)])
@@ -283,7 +322,7 @@ def build(g, T, topo, rank):
         bk = "PS%d" % (4 + p)
         mm([(w5(bk, 256 * i, 256), [(db(2 ** 17), mine("WT", 2 * p + i)), (db(1), mine("KD", 2 * p + i))]) for i in (0, 1)])
         for i in (0, 1):
-            act(w5("G2", 256 * (15 - child(rank, 2 * p + i)), 256), w5(bk, 256 * i, 256), 16384.0)
+            lin("x", w5("G2", 256 * (15 - child(rank, 2 * p + i)), 256), w5(bk, 256 * i, 256), 1.0, 16384.0)
     for p in range(2):
         bk = "PS%d" % (6 + p)
         mm([(v(bk), [(db(256), w5("RM0", 512 * p)), (db(1), w5("RM0", 1024 + 512 * p))])])
@@ -294,7 +333,7 @@ def build(g, T, topo, rank):
            ("WT", T.wt, 0, WTW - 2 * B, 2 * B), ("KD", T.kid, 0, WTW - 2 * B, 2 * B)], came[2:])
     cur[0] = -4
     for p in range(8, -1, -1):
-        widen(w5("N1", 512 * p), w5("N2", own + 512 * ((p + 2) % 4)), P["n1"][p])
+        widen(w5("N1", 512 * p), w5("N2", own + 512 * ((p + 2) % 4)))
 
     def second():
         cur[0] = -2
@@ -304,33 +343,37 @@ def build(g, T, topo, rank):
             lin("a", hi, y, 2.0 ** -30, 2016.5 * 2.0 ** -30)
             bk = xbank()
             mm([(v(bk), [(db(1), y), (db(-2 ** 30), hi)])])
-            lin("x", w5("N2", H * (3 - q) + 512 * p), v(bk), 512.0, 512.0 * 2016)
+            lin("x", w5("N2", HX * (3 - q) + 512 * p), v(bk), 512.0, 512.0 * 2016)
         for n, (s, q, p) in enumerate(pcs):
-            y, wt, hi = w5("LU", 2048 * s + 512 * p), w5("HA", 1024 * s + 512 * p), w5("N2", H * (3 - q) + 1024 + 512 * p)
-            x = 512 * n
+            y, wt, hi = w5("LU", 2048 * s + 512 * p), w5("HA", 1024 * s + 512 * p), w5("N2", HX * (3 - q) + 1024 + 512 * p)
+            x = 512 * (n % 4)
             ts(hi, y, M9, M9 + 16384, ALU.add, ALU.subtract)
             bk = xbank()
             out = [w5("G2", 256 * (15 - child(q, 2 * p + i)), 256) for i in (0, 1)]
-            widen(w5("X32", x), y, P["wx"][n])
-            if P["route"][n] != "V":
-                mm([(v(bk), [(db(-1), hi), (db(2 ** 41), wt), (df(1), w5("X32", x))])])
-                for i in (0, 1):
-                    act(out[i], w5(bk, 256 * i, 256))
-            else:
-                mm([(v(bk), [(db(-1), hi), (db(2 ** 41), wt)])])
-                for i in (0, 1):
-                    tt(out[i], w5("X32", x + 256 * i, 256), w5(bk, 256 * i, 256), ALU.add)
+            widen(w5("X32", x), y)
+            two = [(db(-1), hi), (db(2 ** 41), wt)]
+            pick("V", {"V": [lambda: mm([(v(bk), two)])] +
+                       [lambda i=i: tt(out[i], w5("X32", x + 256 * i, 256), w5(bk, 256 * i, 256), ALU.add) for i in (0, 1)],
+                       "A": [lambda: mm([(v(bk), two + [(df(1), w5("X32", x))])])] +
+                       [lambda i=i: act(out[i], w5(bk, 256 * i, 256)) for i in (0, 1)]})
+        for q in [rank] + peers:
+            widen(w5("N2", HX * (3 - q) + H, HX - H), w5("N2", HX * (3 - q), HX - H), "G")
         cur[0] = -3
         for p in range(4):
-            widen(w5("R2", D * rank + 512 * p), w5("RM0", 512 * p), P["own"][p])
+            widen(w5("R2", D * rank + 512 * p), w5("RM0", 512 * p))
         for n, (s, q, p) in enumerate(pcs):
             y, x = w5("LU", 2048 * s + 1024 + 512 * p), w5("Y32", 512 * (n % 3))
             lin("r", w5("R2", D * q + 512 * p), y, 2.0 ** -8, -127.5 / 256)
-            widen(x, y, P["wid"][n])
+            widen(x, y)
             ts(w5("R2", D * q + 1024 + 512 * p), x, 255, None, ALU.bitwise_and)
 
     def L(name, c, base=0):
         return v(name, base + c * CW, base + (c + 1) * CW)
+
+    def swap(out, terms):
+        n, a0 = out[1][0][:2]
+        return [(w5(n, a0 + 32 * b, 32), [(w5("MS", 128 * (4 * DS.index(k) + 2 * b + a), 128), w5(x[1][0][0], x[1][0][1] + 32 * a, 32))
+                                          for k, x in terms for a in (0, 1)]) for b in (0, 1)]
 
     def sm(c, k):
         return v("PS%d" % (4 + c), k * CW, (k + 1) * CW)
@@ -338,7 +381,7 @@ def build(g, T, topo, rank):
     def kbank(c, i):
         return "PS%d" % (c * (NO // 512) + i)
 
-    def draw(rd, c, wwin, kwin, nwin, ob, oh):
+    def draw(c, wwin, kwin, nwin, ob, oh):
         o0 = c * NO
         ga = "GA" if kwin else "GG"
         for i in range(NO // 512):
@@ -347,94 +390,97 @@ def build(g, T, topo, rank):
             tt(w5("GP", a), ind(nwin, w5(oh, k0, 32)), w5(ga, a), ALU.mult)
         if kwin:
             for i in range(NO // 512):
-                widen(w5("GK", o0 + 512 * i), ind(kwin, w5(ob, c * CW + 32 * i, 32)), P["gk"][4 * rd + 2 * c + i])
+                widen(w5("GK", o0 + 512 * i), ind(kwin, w5(ob, c * CW + 32 * i, 32)), "A")
         parts = [("GA", db(2 ** 26)), ("GP", db(4096)), ("GK", db(1))] if kwin else [("GG", df(2 ** 50)), ("GP", db(2 ** 36))]
         for i in range(NO // 512):
             bk = kbank(c, i)
             for n, (nm, k) in enumerate(parts):
-                for js in ([[0, 1, 2, 3]] if nm != "GG" else P["split"]):
-                    mm([(w5(bk, 128 * j, 128), [(v(nm, o0 + 4 * i + j, o0 + NO, S), k)]) for j in js],
-                       n == 0 and js[0] == 0, n == len(parts) - 1, [(bk, 0, 512)])
+                mm([(w5(bk, 128 * j, 128), [(v(nm, o0 + 512 * i + j, o0 + 512 * i + 512, 4), k)]) for j in range(4)],
+                   n == 0, n == len(parts) - 1, [(bk, 0, 512)])
             scan(w5("SC", o0 + 512 * i), v("DL"), v(bk), ALU.add, ALU.max)
-        ts(w5("QI", 72 * c, 64), v("SC", o0 + 15, o0 + NO, 16), 4095, None, ALU.bitwise_and)
+        win = v("SC", o0 + 15, o0 + NO, 16)
+        ts(w5("QI", 72 * c, 64), win, 4095 if kwin else 127, None, ALU.bitwise_and)
         lin("Q", w5("QB", c * QW + 16, 128), ind(w5("QI", 72 * c, 72), v("OQ")), 1.0, -2048.0)
-        mm([(sm(c, 0), [(w5("QB", c * QW + 16 - S * k, 128), w5("EE", k * CW, CW)) for k in range(NSH)])])
-        lin("e", L("QC", c), sm(c, 0), 1.0, 0.0)
-        return sm(c, 0) if P["ps"] else L("QC", c)
+        if not kwin:
+            ts(w5("QI", 72 * (c + 2), 64), win, 8, 15, ALU.logical_shift_right, ALU.bitwise_and)
+            lin("-", w5("QB", (c + 2) * QW + 16, 128), ind(w5("QI", 72 * (c + 2), 72), v("OQ")), -1.0, 2048.0)
 
-    def goes(rd, c):
-        mm([(sm(c, 3), [(db(1), L("CP", c)), (db(-4), L("UP", c))] + ([(db(8), L("BO", c))] if rd == 2 else []))])
-        a = 4 * CW * c
-        for k in range(4):
-            ts(w5("MK", a + CW * k, CW), sm(c, 3), float(k - 480), None, ALU.is_equal)
-        if c == 0:
-            scan(w5("IK", 0, 4 * CW), w5("RS", 0, 4 * CW), w5("MK", 0, 4 * CW), ALU.mult, ALU.add)
+    def gate(c, k, out, flag, x, op=ALU.mult):
+        if op == ALU.mult:
+            by = [lambda: mm([(sm(c, k), [(db(8192), flag), (df(1) if x[3] == F32 else db(1), x)])]),
+                  lambda: act(out, sm(c, k), -8192.0, 1.0, AF.Relu)]
         else:
-            for k in range(4):
-                b = a + CW * k
-                scan(w5("IK", b, CW), w5("RS", 4 * CW, CW), w5("MK", b, CW), ALU.mult, ALU.add, w5("IK", b - 3 * CW - 1, 1))
-        mm([(w5("PS6", a, 4 * CW), [(v("BLK"), w5("IK", a, 4 * CW)), (v("UT"), w5("MK", a, 4 * CW))])])
-        act(w5("SG", a, 4 * CW), w5("PS6", a, 4 * CW), CAP + 0.5 - 4096, -1.0, AF.Sign)
-        mm([(sm(c, 3), [(db(1), w5("SG", a + CW * k, CW)) for k in range(4)])])
-        act(L("GS", c), sm(c, 3))
+            by = [lambda: mm([(sm(c, k), [(df(1), flag), (df(1), x)])]), lambda: act(out, sm(c, k))]
+        pick(P["gate"], {"A": by, "V": [None, lambda: tt(out, flag, x, op)]})
 
-    CD = 32768 + 2 * 327680 + 160 - 1310720 + 15 + 3 * 2048
+    def turn(c, e):
+        return [(w5("QB", c * QW + 16 - 4 * k, 128), w5(e, k * CW, CW)) for k in range(2)]
+
+    def goes(rd):
+        for c in range(NC):
+            x = L("PS7", c, 128)
+            mm(([(x, [(db(8), L("BO", c))])] if rd == 2 else []) + swap(x, [(1, L("CP", c)), (-4, L("UP", c))]), True, True)
+        for k in range(4):
+            ts(w5("MK", 128 * k, 128), w5("PS7", 128, 128), float(k - 480), None, ALU.is_equal)
+        scan(v("IK"), v("RS"), v("MK"), ALU.mult, ALU.add)
+        mm([(v("PS6"), [(v("BLK"), v("IK")), (v("UT"), v("MK"))])])
+        act(v("SG"), v("PS6"), CAP + 0.5 - 4096, -1.0, AF.Sign)
+        mm([(w5("PS7", 128, 128), [(db(1), w5("SG", 128 * k, 128)) for k in range(4)])])
+        lin("x", v("GS"), w5("PS7", 128, 128), 1.0, 0.0)
+
+    CD = 32768 - 2048 + 15 + 3 * 2048
+    cur[0] = -1
+    for c in range(NC):
+        mm(swap(sm(c, 7), [(1, L("BS", c))]))
+        lin("x", L("BY", c), sm(c, 7), 1.0, 0.0)
     for rd in range(RO):
         for c in range(NC):
             cur[0] = c
             if rd == 0:
-                q = draw(rd, c, v("WT", 0, B), v("KD", 0, B), w5("N2", own, H), "OB", "OH")
+                draw(c, v("WT", 0, B), v("KD", 0, B), w5("N2", own, H), "OB", "OH")
             else:
                 w = WT1 if rd == 1 else WTW
-                q = draw(rd, c, v("WT", 0, w), v("KD", 0, w), v("N1"), "OB", "OH")
-            lin("o", L("OB2", c), q, 1.0, 2048.0)
-            lin("p", L("CP", c), q, 1 / 256, 167.5 + 1 / 512)
-            lin("u", L("UP", c), q, 1 / 1024, 161.5 + 1 / 2048)
-            base = [(db(1), L("BS", c))] + ([(dh(611), L("TT", c, 128 * (rd - 1)))] if rd else []) + [(dh(592), L("QC", c))]
-            mm([(sm(c, 1), base + [(db(-37), L("CP", c))])])
-            lin("h", L("H2", c), sm(c, 1), 2.0 ** -35, 0.0)
-            mm([(sm(c, 2), base + [(dh(2011), L("CP", c)), (db(-8192), L("UP", c)), (db(-2 ** 35), L("H2", c))])])
-            lin("H", L("OH2", c), sm(c, 2), 1.0, 1023.5 + 983040)
-            if rd:
-                goes(rd, c)
+                draw(c, v("WT", 0, w), v("KD", 0, w), v("N1"), "OB", "OH")
+            x = L("PS7", c)
+            mm([(sm(c, 0), turn(c, "EE"))])
+            mm([(x, [(db(1), L("BY", c))])] + (swap(x, [(611, L("TT", c, 128 * (rd - 1)))]) if rd else []) + [(x, turn(c, "E5"))], True, True)
+            lin("o", L("OB2", c), sm(c, 0), 1.0, 2048.0)
+            lin("h", L("H2", c), x, 1.0, 2.0 ** 21 + 1023.5)
+            ts(L("H3", c), L("H2", c), H - 1, None, ALU.bitwise_and)
+            lin("p", L("CP", c), sm(c, 0), 1 / 256, 167.5 + 1 / 512)
+            lin("u", L("UP", c), sm(c, 0), 1 / 1024, 161.5 + 1 / 2048)
+            mm([(sm(c, 2), [(db(1), v("CC", 0, 64)), (db(HX), v("CC", 64, 128)), (db(-37), L("CP", c)), (db(HX), L("CP", c)),
+                            (db(-4 * HX), L("UP", c))])])
+            tt(L("OH2", c), L("H3", c), sm(c, 2), ALU.add)
         if rd == 0:
             second()
-            for c in range(NC):
-                cur[0] = c
-                goes(rd, c)
+        cur[0] = 1
+        goes(rd)
         for c in range(NC):
             cur[0] = c
             o0 = c * NO
-            q = draw(rd, c, v("G2"), None, v("N2"), "OB2", "OH2")
-            lin("P", L("CP2", c), q, 1 / 256, 167.5 + 1 / 512)
-            lin("c", L("CQ", c), q, 1 / 128, 175.5 + 1 / 256)
-            mm([(sm(c, 4), [(db(-2048), L("CP", c)), (db(8192), L("UP", c)), (dh(16), L("QC", c)),
-                            (db(-1), L("CP2", c)), (db(-2048), L("CQ", c))])])
+            draw(c, v("G2"), None, v("N2"), "OB2", "OH2")
+            mm([(sm(c, 4), [(db(-2048 * k), L("MK", c, 128 * k)) for k in (1, 2, 3)] + turn(c, "E6") + turn(c + 2, "EE"))])
             lin("d", L("OR", c), sm(c, 4), 1.0, CD)
-            act(L("DV", c), sm(c, 4), CD + 1)
+            lin("x", L("DV", c), sm(c, 4), 1.0, CD + 1)
             for i in range(NO // 512):
                 a = o0 + 512 * i
                 gi = ind(v("R2"), w5("OR", c * CW + 32 * i, 32))
-                if P["room"][(rd * NC + c) * 2 + i] == "A":
-                    act(w5("GK", a), gi)
-                    mm([(v(kbank(c, i)), [(db(1), w5("ND0", a)), (db(-1), w5("GK", a))])])
-                    act(w5("VI", a), v(kbank(c, i)), 0.0, 1.0, AF.Relu)
-                else:
-                    tt(w5("VI", a), gi, w5("ND0", a), ALU.is_lt)
+                bk = v(kbank(c, i))
+                by = [lambda: act(w5("GK", a), gi), lambda: mm([(bk, [(db(1), w5("ND0", a)), (db(-1), w5("GK", a))])])]
+                pick(P["room"][(rd * NC + c) * 2 + i], {"A": by + [lambda: act(w5("VI", a), bk, 0.0, 1.0, AF.Relu)],
+                                                        "V": [None, None, lambda: tt(w5("VI", a), gi, w5("ND0", a), ALU.is_lt)]})
             terms = [(db(-1), L("GS", c))]
             if rd:
                 tt(L("EQ", c), L("DV", c), L("KV", c) if rd == 1 else L("S12", c), ALU.is_equal)
                 terms.append((db(1), L("EQ", c)))
             if rd == 2:
-                tt(L("DA", c), L("DV", c), L("NN", c), ALU.mult)
-                tt(L("DBB", c), L("DV", c), L("DA", c), ALU.subtract)
+                gate(c, 6, L("DA", c), L("NN", c), L("DV", c))
+                gate(c, 7, L("DBB", c), L("NM", c), L("DV", c))
             terms += [(w5("SEL", 15 - r, 128), v("VI", o0 + r, o0 + NO, 16)) for r in range(16)]
             mm([(sm(c, 5), terms)])
             kp = L("KP", c, 128 * rd)
-            if "k" in P["act"]:
-                act(kp, sm(c, 5), 3.0, -1.0, AF.Relu)
-            else:
-                ts(kp, sm(c, 5), 2.5, None, ALU.is_le)
+            pick("A", {"A": lambda: act(kp, sm(c, 5), 3.0, -1.0, AF.Relu), "V": lambda: ts(kp, sm(c, 5), 2.5, None, ALU.is_le)})
             if rd < 2:
                 up = ([L("TT", c)] if rd else []) + [L("GS", c)]
                 mm([(sm(c, 6), [(db(1), L("BB", c))] + [(dh(1237), x) for x in up] + [(dh(-1237), kp)]),
@@ -442,19 +488,20 @@ def build(g, T, topo, rank):
                 lin("b", L("OB", c), sm(c, 6), 1.0, 2048.0 + 4 * 1237)
                 lin("n", L("OH", c), sm(c, 7), 1.0, 1024.0 - 4 * 724 + 3072)
                 mm([(sm(c, 1), [(db(1), x) for x in up] + [(db(-1), kp)])])
-                act(L("TT", c, 128 * rd), sm(c, 1), 4.0)
-                tt(L("KV", c, 128 * rd), kp, L("DV", c), ALU.mult)
+                lin("x", L("TT", c, 128 * rd), sm(c, 1), 1.0, 4.0)
+                gate(c, 3, L("KV", c, 128 * rd), kp, L("DV", c))
             if rd == 1:
-                tt(L("BO", c), L("KP", c), kp, ALU.mult)
-                tt(L("S12", c), L("KV", c), L("KV", c, 128), ALU.add)
-                tt(L("U1", c), L("KP", c), L("KV", c, 128), ALU.mult)
+                gate(c, 3, L("BO", c), L("KP", c), kp)
+                gate(c, 3, L("S12", c), L("KV", c), L("KV", c, 128), ALU.add)
+                gate(c, 3, L("U1", c), L("KP", c), L("KV", c, 128))
                 tt(L("U2", c), L("S12", c), L("U1", c), ALU.subtract)
                 act(L("B12", c), L("U1", c), -1.0)
                 act(L("A12", c), L("U2", c), -1.0)
                 act(L("NN", c), L("S12", c), 1.0, -1.0, AF.Relu)
+                lin("x", L("NM", c), L("NN", c), -1.0, 1.0)
             if rd == 2:
                 for y, dst, dv, old, tmp in (("YA", T.ya, "DA", "A12", "U1"), ("YB", T.yb, "DBB", "B12", "U2")):
-                    tt(L(tmp, c), kp, L(dv, c), ALU.mult)
+                    gate(c, 1 + (y == "YA"), L(tmp, c), kp, L(dv, c))
                     tt(L(y, c), L(tmp, c), L(old, c), ALU.add)
                     dma(dst[:, c * CW:(c + 1) * CW], L(y, c)[0], 128 * CW * 4, L(y, c)[1], [])
     return ops, nsent
@@ -472,6 +519,9 @@ def schedule(ops):
         for b in o["banks"]:
             o["deps"] |= set(j for q, j in last.get(b, {}).items() if q != o["q"])
             last.setdefault(b, {})[o["q"]] = i
+        for d in list(o["deps"]):
+            if ops[d]["kind"] == "n":
+                o["deps"] = (o["deps"] - {d}) | ops[d]["deps"]
     return order
 
 
@@ -486,7 +536,7 @@ def rank_program(g, core, T, topo):
     seen = {}
     for i in order:
         o = ops[i]
-        if o["kind"] == "x":
+        if o["kind"] in "xn":
             continue
         need = {}
         for d in o["deps"]:

from concourse.bass import DstId, RemoteDMATransfer
from concourse.mybir import AluOpType as ALU, ActivationFunctionType as AF

NR, B, H, D, O, CAP, RO = 4, 4096, 2048, 2048, 2048, 512, 3
NC = 2
CW = 128 // NC
NO = O // NC
QW = 144
P = {"room": "VVVVVVVVVAVA", "gate": "V", "banks": "767676012301", "act": "xyzrdbnkQoup", "rm": 1, "nd": 1}
M9 = 1.5 * 2.0 ** 32
WTW, WT1, HX = 9056, 6576, 2608
DB = [1, -1, 64, 512, 256, 2 ** 17, 4096, 2 ** 26, 2 ** 36, 2 ** 41, -2 ** 30, -37, 8,
      -2048, 2608, -10432, -4096, -6144, 8192]
DH = [1237, -1237, -724, 724]
DS = [1, -4, 611]
DF = [1, 2 ** 50]

BF, F16, F32, I32, U16 = "bfloat16", "float16", "float32", "int32", "uint16"
SB = {
    "WT": (WTW, BF), "KD": (WTW, BF), "N1": (5120, BF), "NR0": (H, BF), "RM0": (D, BF), "ND0": (O, BF),
    "G2": (B, F32), "N2": (NR * HX, BF), "R2": (NR * D, I32), "XU": (2048, U16), "XH": (1024, F16),
    "LU": (6144, U16), "LH": (3072, F16), "HA": (3072, F16), "X32": (2048, F32), "Y32": (1536, I32),
    "GA": (O, BF), "GK": (O, BF), "GG": (O, F32), "GP": (O, F16), "VI": (O, BF),
    "SC": (O, I32), "QI": (4 * 72, I32), "QB": (4 * QW, F16),
    "BEG": (128, I32), "SAL": (128, I32), "I1": (128, I32), "I2": (128, I32), "I3": (128, I32), "I4": (128, I32),
    "F1": (128, F32), "BB": (128, F16), "BA": (128, F16), "BS": (128, F16), "BY": (128, F16), "CC": (128, F16),
    "OB": (128, U16), "OH": (128, U16), "OB2": (128, U16), "OH2": (128, U16), "OR": (128, U16), "OQ": (8, U16),
    "H2": (128, I32), "H3": (128, I32),
    "CP": (128, BF), "UP": (128, BF), "MK": (512, BF), "IK": (512, BF), "SG": (512, BF),
    "RS": (512, BF), "DL": (512, BF), "GS": (128, BF), "TT": (256, BF), "KP": (384, BF),
    "EQ": (128, BF), "BO": (128, BF), "NN": (128, BF), "NM": (128, BF),
    "DV": (128, F32), "KV": (256, F32), "S12": (128, F32), "B12": (128, F32), "A12": (128, F32), "U1": (128, F32),
    "U2": (128, F32), "DA": (128, F32), "DBB": (128, F32), "YA": (128, F32), "YB": (128, F32),
    "ONE": (144, F32), "EE": (128, BF), "E5": (128, F16), "E6": (128, BF),
    "PI": (2, I32), "PJ": (4, I32), "PF": (8, F32), "SH": (256, BF), "MS": (128 * 12, F16),
    "JF": (144, F32), "MF": (128, F32), "OF": (8, F32), "OG": (8, F32),
    "SEL": (144, BF), "BLK": (128, BF), "UT0": (128, BF), "UT": (128, BF),
    "MB": (128 * len(DB), BF), "MH": (128 * len(DH), F16), "MFF": (128 * len(DF), F32),
}
SCRATCH = {k: ("sbuf", [128, w], t) for k, (w, t) in SB.items()}
for _i in range(8):
    SCRATCH["PS%d" % _i] = ("psum", [128, 512], F32)
SEMAPHORES = ["cV", "cA", "cP", "cG", "sent"] + ["dm%d" % i for i in range(24)] + ["ar%d" % i for i in range(12)]

CY, PCY, GF, RATE = 0.83e-3 * 1.1, 0.0005 * 1.1, 1.56, 250e3
ENGINE = "AAAAAAAAAAVAVAAAAAVAVAAVGVVVAVAGAAAVAVAAGAGGGGGVVAVAVVVVAAVAVAVVAVAAAAAVAVAAVAVGVAVAVAVGGGGGGGGAGAAAAAGAGAGAAAAAVVAAAAVAAAAVVAAAAVVVAAVAAAAAAAAAAAAAAVAAAAAVVVAAVAAAVVVAAAVAVVAVAAVAVVAAAAAAAAAAAAVAVVAVVAAVVVVVAAVA"
ORDER = "00050y01060203040B0z0A0C0D070G0d0a0u0K0Y0E1b0m0j0F0N090b0e0p0c0J0Z0v0h080H0L160I1d0X110O0P1o1p1f0g1j0t1l1e240w181g12170r0n14293Q26130o0S1m1n250l0M1a0k1c1h1k1q1s151i190i0R0V1r2g2h2H1t2i2F0Q0T0U2I2m2P282q1A1I2Q1y1L1B2K1u272a1w1v1x1H2b2l2j0x2r2k1K2J2R2G0q1z1N2S2n2o2e2s231C1G3U2L2c2M2N1O2f2p0s2t1Q1J3d0f1P2O2u0W2d1M2T371R3g2U102v343j1S1E3X3x1D38392w2x2W2z2Y3a2V3e353s1F1W3n363C3r3B3m3t3o3b3f3c2B3L3w2X3G3D3y3h3v3p3q3u3M303H3N3I3k1T1U1V1X1Y1Z2120223i42453R3V3l3E3F2Z2C2A3z3A2y313O3P3J3K324g4h2D3S3Z4r4t4X4Z4d3Y4a47443T43464j2E4l40334k4i4s4e4u4b4v4y544z4w5141483W4Y504f4c4A4x4m524D4B535556494C4E4n4F4G4o4L4M4I4J57594N4K4p585a4H5b4q5c4O5h5e5f5i5d5j5g4P4Q4V5k4R4S5v4T5l5D5m5t5n4U5x5y5w5u5U5z5o5E5F5S5V5X5A5p5B6263645Y5G5C5H5W5T5I5r5q5J5K5Z5L5O5P6s655M6u5N6061665Q6h6w5s5R674W6v6t686z6d6e6A696a7a6x6b6f6i7c6B6c6y6g6k6l6E6C7b6m6j7d6n6D6F7e7h6G7f7i6o6H6I6M6p6J6K6N6q7g7j6P7k7m7n6O7l7o6L6r7p7q6Q7u7v7r7s6R6X6S7w7x7t7y6T6U6Y7W7S7U7z6Z7T7V7F707G6V7Y7X7D7A7Z80827B7C7181728384858j8h867H738r7I7J8k6W878m8n88898s8l7E8b8t8i8a8e8d8u8c7K8T7L8o8p8f8G8R8q8g7M8v8Y8U8w748x8y8S7Q7O768C8D8Z8A8E8H8z789v9t797R8V8W8B908J758L8I8F8K9w8X7N9391777P9A9x9B9492959u8M9C9y9z96979F9D98999b9G9E8N9c9H8O9h8P9a9e9J9I9d8Q9N9O9K9L9T9U9Q9M9P9R9f9i9g9S9j9k9V9l9p9W9q9m9Xa1a29r9Y9n9Za39s9oa0a4"


def build(g, T, topo, rank):
    ops = []
    acc = {}
    cur = [-1]
    dry = []

    def v(name, a=0, b=None, step=1):
        if b is None:
            b = T[name].shape[1]
        ap = T[name][:, a:b] if step == 1 else T[name][:, a:b:step]
        return (ap, [(name, a, b)], len(range(a, b, step)), SB[name][1] if name in SB else F32)

    def ind(win, off):
        return (win[0].indirect(off[0]), win[1] + off[1], 16 * off[2], win[3], True)

    def add(q, fn, dur, reads, writes, kind="c", extra=()):
        if dry:
            dry[-1].append((q, fn, dur, reads, writes))
            return None
        i = len(ops)
        deps = set(extra)
        for (n, a, b) in reads:
            for (j, a2, b2, w) in acc.get(n, []):
                if w and a < b2 and a2 < b:
                    deps.add(j)
        for (n, a, b) in writes:
            for (j, a2, b2, w) in acc.get(n, []):
                if a < b2 and a2 < b:
                    deps.add(j)
        for (n, a, b) in writes:
            acc[n] = [e for e in acc.get(n, []) if not (a <= e[1] and e[2] <= b)] + [(i, a, b, True)]
        for (n, a, b) in reads:
            acc.setdefault(n, []).append((i, a, b, False))
        deps.discard(i)
        banks = set(n for (n, a, b) in reads + writes if n.startswith("PS"))
        ops.append({"q": q, "fn": fn, "dur": dur, "deps": deps, "kind": kind, "banks": banks, "c": cur[0],
                    "g": int(any(n.startswith("O") and n[1] in "BHRQ" for (n, a, b) in reads))})
        return i

    def vcost(out, ins, tt=False):
        n = out[2]
        if len(ins[0]) == 5:
            return 0.05 + n * GF * CY
        f = 0.5 if (all(x[3] in (BF, F16, U16) for x in [out] + ins) and not tt) else 1.0
        if tt and not any(x[1][0][0].startswith("PS") for x in ins):
            f = 2.0
        return max(64, n * f) * CY + 0.03

    def ts(out, in0, s1, s2, op0, op1=None):
        r = in0[1] + (s1[1] if isinstance(s1, tuple) else [])
        a1 = s1[0] if isinstance(s1, tuple) else s1
        if op1 is None:
            fn = lambda: g.vector.tensor_scalar(out[0], in0[0], a1, None, op0)
        else:
            fn = lambda: g.vector.tensor_scalar(out[0], in0[0], a1, s2, op0, op1)
        return add("V", fn, vcost(out, [in0]), r, out[1])

    def tt(out, in0, in1, op):
        return add("V", lambda: g.vector.tensor_tensor(out[0], in0[0], in1[0], op), vcost(out, [in0, in1], True),
                   in0[1] + in1[1], out[1])

    def cp(out, in0):
        return add("V", lambda: g.vector.tensor_copy(out[0], in0[0]), vcost(out, [in0]), in0[1], out[1])

    def ms(out, c):
        return add("V", lambda: g.vector.memset(out[0], c), vcost(out, [out]), [], out[1])

    def scan(out, d0, d1, op0, op1):
        return add("V", lambda: g.vector.tensor_tensor_scan(out[0], d0[0], d1[0], 0.0, op0, op1),
                   vcost(out, [d0, d1]), d0[1] + d1[1], out[1])

    def act(out, in0, bias=0.0, scale=1.0, func=AF.Identity):
        d = 0.065 + out[2] * GF * CY if len(in0) == 5 else max(64, out[2]) * CY + 0.03
        return add("A", lambda: g.scalar.activation(out[0], in0[0], func, bias=float(bias), scale=float(scale)), d, in0[1], out[1])

    npick = [0]

    def pick(on, ways):
        npick[0] += 1
        on = ENGINE[npick[0] - 1] if ENGINE else on
        rec = {}
        for k, fs in ways.items():
            rec[k] = []
            for f in fs if isinstance(fs, list) else [fs]:
                dry.append([("X", None, 0.0, [], [])])
                if f:
                    f()
                rec[k].append(dry.pop()[-1])
        for n, (q, fn, dur, _, _) in enumerate(rec[on]):
            i = add(q, fn, dur, sum((r[n][3] for r in rec.values()), []), sum((r[n][4] for r in rec.values()), []), "c" if fn else "n")
            ops[i]["alt"] = {k: (r[n][0], r[n][2], set(x[0] for x in r[n][3] + r[n][4] if x[0].startswith("PS")),
                                 int(any(x[0][0] == "O" and x[0][1] in "BHRQ" for x in r[n][3]))) for k, r in rec.items()}
            ops[i]["grp"], ops[i]["on"] = npick[0] - 1, on
            ops[i]["banks"], ops[i]["g"] = ops[i]["alt"][on][2:]
        return i

    def lin(tag, out, in0, scale, bias):
        return pick("A" if tag in P["act"] else "V", {"A": lambda: act(out, in0, bias, scale),
                    "V": lambda: ts(out, in0, float(scale), float(bias), ALU.mult, ALU.add)})

    def mm(groups, first=None, end=None, more=()):
        r, w, d = [], list(more), 0.03
        for out, terms in groups:
            w += out[1]
            for l, x in terms:
                r += l[1] + x[1]
                d += max(min(64, l[2]), x[2]) * (4 if l[3] == F32 else 1) * PCY

        def fn():
            last = None
            for n, (out, terms) in enumerate(groups):
                for k, (l, x) in enumerate(terms):
                    last = g.tensor.matmul(out[0], l[0], x[0], k == 0 if first is None else (first and n == k == 0),
                                           k == len(terms) - 1 and (end is None or (end and n == len(groups) - 1)))
            return last
        return add("P", fn, d, r, w)

    def iota(out, pat, base, mult):
        kw = {} if out[3] == I32 else {"allow_small_or_imprecise_dtypes": True}
        return add("G", lambda: g.iota(out[0], pat, base, mult, **kw), 0.13 + 2 * out[2] * CY, [], out[1])

    def asel(out, in0, pat, op, base, mult):
        return add("G", lambda: g.affine_select(out[0], in0[0], pat, op, 0.0, base, mult), 0.17 + 2 * out[2] * CY, in0[1], out[1])

    def widen(out, in0, on="G"):
        ways = {"A": lambda: act(out, in0), "V": lambda: cp(out, in0)}
        if len(in0) == 4:
            ways["G"] = lambda: asel(out, in0, [[0, out[2]]], ALU.is_ge, 0, 0)
        return pick(on, ways)

    nd = [0]

    def dma(out, in_, nbytes, reads, writes, extra=()):
        i = add("S", lambda: g.sync.dma_start(out, in_), nbytes / RATE, reads, writes, "d", extra)
        ops[i]["sem"] = (T.sem["dm%d" % nd[0]], 16)
        nd[0] += 1
        return i

    def db(c):
        return v("MB", 128 * DB.index(c), 128 * DB.index(c) + 128)

    def dh(c):
        return v("MH", 128 * DH.index(c), 128 * DH.index(c) + 128)

    def df(c):
        return v("MFF", 128 * DF.index(c), 128 * DF.index(c) + 128)

    def w5(name, a, n=512):
        return v(name, a, a + n)

    prev = []

    def loads(lst, extra=()):
        for name, src, a, b, at in lst:
            i = dma(v(name, at, at + b - a)[0], src[:, a:b], 128 * (b - a) * (4 if b == 128 else 2), [], [(name, at, at + b - a)], extra)
            ops[i]["after"] = prev[-1:] if len(prev) < 5 else prev[4:5]
            prev.append(i)
    loads([("NR0", T.noise, 0, H, 0), ("BEG", T.begin, 0, 128, 0), ("SAL", T.salt, 0, 128, 0), ("WT", T.wt, 0, B, 0), ("KD", T.kid, 0, B, 0)])

    ms(v("ONE"), 1.0)
    asel(df(1), v("ONE", 0, 128), [[-1, 128]], ALU.is_equal, 0, 1)
    cp(db(1), df(1))
    for n, c in enumerate(DB[1:]):
        lin("x" if n % 3 == 2 else "-", db(c), db(1), c, 0.0)
    for c in DH:
        lin("-", dh(c), db(1), c, 0.0)
    for c in DF[1:]:
        act(df(c), df(1), 0.0, c)
    asel(v("EE"), v("ONE", 0, 128), [[-1, 2], [-2, 2], [-4, 32]], ALU.is_equal, 0, 1)
    lin("-", v("E5"), v("EE"), 592.0, 0.0)
    lin("-", v("E6"), v("EE"), 16.0, 0.0)
    iota(v("PI", 0, 1), [[0, 1]], 0, 1)
    ts(v("PJ", 0, 1), v("PI", 0, 1), 112, None, ALU.bitwise_and)
    for n, m in enumerate((3, 4, 8)):
        ts(v("PJ", n + 1, n + 2), v("PI", 0, 1), m, None, ALU.bitwise_and)
    cp(v("PF", 0, 4), v("PJ"))
    ts(v("PF", 4, 5), v("PF", 3, 4), 0.125, None, ALU.mult)
    ts(v("PF", 5, 6), v("PF", 4, 5), -1.0, 1.0, ALU.mult, ALU.add)
    ts(v("PF", 6, 7), v("PF", 2, 3), 8.0, v("PF", 1, 2)[0], ALU.mult, ALU.add)
    ops[-1]["deps"].add(len(ops) - 4)
    ts(v("PF", 7, 8), v("PF", 6, 7), v("PF", 3, 4), 8.0, ALU.add, ALU.mult)
    ts(v("PF", 1, 2), v("PF", 3, 4), -4.0, v("PF", 7, 8)[0], ALU.mult, ALU.add)
    ops[-1]["deps"].add(len(ops) - 2)
    asel(v("SH", 0, 128), v("ONE", 0, 128), [[-1, 128]], ALU.is_equal, 8, 1)
    asel(v("SH", 128, 256), v("ONE", 0, 128), [[-1, 128]], ALU.is_equal, -8, 1)
    for n, k in enumerate(DS):
        for b in (0, 1):
            for a in (0, 1):
                ts(w5("MS", 128 * (4 * n + 2 * b + a), 128), db(1) if a == b else w5("SH", 128 * b, 128), v("PF", 5 - b, 6 - b),
                   float(k), ALU.mult, ALU.mult)
    iota(v("JF"), [[1, 144]], -15, 0)
    iota(v("MF"), [[16, 8], [0, 16]], 0, 0)
    iota(v("OF"), [[1, 8]], 0, 0)
    ts(v("SEL"), v("JF"), v("PF", 0, 1), None, ALU.is_equal)
    ts(v("BLK"), v("MF"), v("PF", 0, 1), None, ALU.is_equal)
    ts(v("OG"), v("OF"), v("PF", 1, 2), 64.0, ALU.add, ALU.min)
    cp(v("OQ"), v("OG"))
    asel(v("UT0"), v("BLK"), [[-1, 128]], ALU.is_gt, 0, 1)
    tt(v("UT"), db(-4096), v("UT0"), ALU.subtract)
    ms(v("DL"), 256.0)
    ms(v("DL", 0, 512, 16), -2.0 ** 24)
    ms(v("RS"), 1.0)
    ms(v("RS", 0, 512, 128), 0.0)
    ms(v("QB"), 0.0)
    ms(v("CC", 0, 64), 555.0 + 37 * 160 - 2 * HX)
    ms(v("CC", 64, 128), 482.0)
    ms(v("QI"), 2048)

    widen(v("OB"), v("BEG"), "A")
    act(v("F1"), v("BEG"), 0.0, 37.0)
    tt(v("I1"), v("F1"), v("SAL"), ALU.add)
    ts(v("I2"), v("I1"), H - 1, None, ALU.bitwise_and)
    cp(v("OH"), v("I2"))
    act(v("BB"), v("BEG"), -2048.0)
    act(v("BA"), v("I2"), -1024.0)
    act(v("I3"), v("SAL"), 0.0)
    ts(v("I4"), v("I3"), H - 1, None, ALU.bitwise_and)
    act(v("BS"), v("I4"), -1023.5)

    xb = [0]

    def xbank():
        xb[0] += 1
        return "PS" + P["banks"][(xb[0] - 1) % len(P["banks"])]

    peers = [q for q in range(NR) if q != rank]
    came = []

    def send(k, src, land, width, at):
        mask = topo.mask(T.cores[rank], T.cores[peers[0]])
        per = len(topo.engines(T.cores[rank], T.cores[peers[0]]))

        def fn():
            ids, dsts = [], []
            for q in peers:
                rid, pid, _ = topo.addr(T.cores[q])
                a = width * [x for x in range(NR) if x != q].index(rank) + at
                ids.append(DstId(rid=rid, pnc=pid))
                dsts.append(T[land][:, a:a + 1024])
            tr = RemoteDMATransfer(dst_ids=ids, dma_engine_mask=mask, remote_sem=T.sem["ar%d" % (3 * rank + k)],
                                   src=src[0], dsts=dsts)
            return g.remote_dma_fused([tr], local_sem=T.sem.sent)
        i = add("G", fn, 3 * 128 * 2048 / RATE, src[1], [], "r")
        for s, q in enumerate(peers):
            j = add("X", None, 0.5, [], [(land, width * s + at, width * s + at + 1024)], "x", [i])
            ops[j]["sem"] = (T.sem["ar%d" % (3 * q + k)], per)
        came.append(j)
        return per

    def child(r, i):
        return 12 + r - 4 * i

    def mine(name, i):
        return v(name, child(rank, i), B, 16)

    own = HX * (3 - rank)
    for p in range(2):
        lin("-", w5("N2", own + 1024 * p, 1024), w5("NR0", 1024 * p, 1024), 512.0, -16384.0)
    for p in range(2):
        bk = "PS%d" % (4 + p)
        mm([(w5(bk, 256 * i, 256), [(db(64), mine("WT", 2 * p + i)), (db(1), w5("NR0", 512 * p + 256 * i, 256))]) for i in (0, 1)])
        lin("xX"[p], w5("XH", 512 * p), v(bk), 1.0, -2048.0)
    nsent = send(0, v("XH"), "LH", 1024, 0)
    for p in range(2):
        bk = "PS%d" % (6 + p)
        mm([(w5(bk, 256 * i, 256), [(db(512), w5("NR0", 1024 + 512 * p + 256 * i, 256)), (db(1), mine("KD", 2 * p + i))]) for i in (0, 1)])
        e = lin("yY"[p], w5("XU", 512 * p), v(bk), 1.0, 0.0)
    nsent += send(1, w5("XU", 0, 1024), "LU", 2048, 0)
    j = widen(w5("N1", 512 * 9, 512), w5("N2", own + 512 * 3))
    ops[j]["after"] = [came[1] - 3]
    loads([("RM0", T.room, 0, D, 0)], [[e], [j]][P["rm"] - 1])
    for p in range(2):
        bk = "PS%d" % (4 + p)
        mm([(w5(bk, 256 * i, 256), [(db(2 ** 17), mine("WT", 2 * p + i)), (db(1), mine("KD", 2 * p + i))]) for i in (0, 1)])
        for i in (0, 1):
            lin("x", w5("G2", 256 * (15 - child(rank, 2 * p + i)), 256), w5(bk, 256 * i, 256), 1.0, 16384.0)
    for p in range(2):
        bk = "PS%d" % (6 + p)
        mm([(v(bk), [(db(256), w5("RM0", 512 * p)), (db(1), w5("RM0", 1024 + 512 * p))])])
        lin("zZ"[p], w5("XU", 1024 + 512 * p), v(bk), 1.0, 0.0)
    nsent += send(2, w5("XU", 1024, 1024), "LU", 2048, 1024)
    loads([("ND0", T.need, 0, O, 0)], came[P["nd"]:P["nd"] + 1])
    loads([("WT", T.wt, 0, WT1 - B, B), ("KD", T.kid, 0, WT1 - B, B), ("WT", T.wt, WT1 - B, B, WT1), ("KD", T.kid, WT1 - B, B, WT1),
           ("WT", T.wt, 0, WTW - 2 * B, 2 * B), ("KD", T.kid, 0, WTW - 2 * B, 2 * B)], came[2:])
    cur[0] = -4
    for p in range(8, -1, -1):
        widen(w5("N1", 512 * p), w5("N2", own + 512 * ((p + 2) % 4)))

    def second():
        cur[0] = -2
        pcs = [(s, q, p) for s, q in enumerate(peers) for p in range(2)]
        for s, q, p in pcs:
            y, hi = w5("LH", 1024 * s + 512 * p), w5("HA", 1024 * s + 512 * p)
            lin("a", hi, y, 2.0 ** -30, 2016.5 * 2.0 ** -30)
            bk = xbank()
            mm([(v(bk), [(db(1), y), (db(-2 ** 30), hi)])])
            lin("x", w5("N2", HX * (3 - q) + 512 * p), v(bk), 512.0, 512.0 * 2016)
        for n, (s, q, p) in enumerate(pcs):
            y, wt, hi = w5("LU", 2048 * s + 512 * p), w5("HA", 1024 * s + 512 * p), w5("N2", HX * (3 - q) + 1024 + 512 * p)
            x = 512 * (n % 4)
            ts(hi, y, M9, M9 + 16384, ALU.add, ALU.subtract)
            bk = xbank()
            out = [w5("G2", 256 * (15 - child(q, 2 * p + i)), 256) for i in (0, 1)]
            widen(w5("X32", x), y)
            two = [(db(-1), hi), (db(2 ** 41), wt)]
            pick("V", {"V": [lambda: mm([(v(bk), two)])] +
                       [lambda i=i: tt(out[i], w5("X32", x + 256 * i, 256), w5(bk, 256 * i, 256), ALU.add) for i in (0, 1)],
                       "A": [lambda: mm([(v(bk), two + [(df(1), w5("X32", x))])])] +
                       [lambda i=i: act(out[i], w5(bk, 256 * i, 256)) for i in (0, 1)]})
        for q in [rank] + peers:
            widen(w5("N2", HX * (3 - q) + H, HX - H), w5("N2", HX * (3 - q), HX - H), "G")
        cur[0] = -3
        for p in range(4):
            widen(w5("R2", D * rank + 512 * p), w5("RM0", 512 * p))
        for n, (s, q, p) in enumerate(pcs):
            y, x = w5("LU", 2048 * s + 1024 + 512 * p), w5("Y32", 512 * (n % 3))
            lin("r", w5("R2", D * q + 512 * p), y, 2.0 ** -8, -127.5 / 256)
            widen(x, y)
            ts(w5("R2", D * q + 1024 + 512 * p), x, 255, None, ALU.bitwise_and)

    def L(name, c, base=0):
        return v(name, base + c * CW, base + (c + 1) * CW)

    def swap(out, terms):
        n, a0 = out[1][0][:2]
        return [(w5(n, a0 + 32 * b, 32), [(w5("MS", 128 * (4 * DS.index(k) + 2 * b + a), 128), w5(x[1][0][0], x[1][0][1] + 32 * a, 32))
                                          for k, x in terms for a in (0, 1)]) for b in (0, 1)]

    def sm(c, k):
        return v("PS%d" % (4 + c), k * CW, (k + 1) * CW)

    def kbank(c, i):
        return "PS%d" % (c * (NO // 512) + i)

    def draw(c, wwin, kwin, nwin, ob, oh):
        o0 = c * NO
        ga = "GA" if kwin else "GG"
        for i in range(NO // 512):
            a, k0 = o0 + 512 * i, c * CW + 32 * i
            act(w5(ga, a), ind(wwin, w5(ob, k0, 32)), 0.0 if kwin else -2.0 ** -36, 1 / 512 if kwin else 2.0 ** -50)
            tt(w5("GP", a), ind(nwin, w5(oh, k0, 32)), w5(ga, a), ALU.mult)
        if kwin:
            for i in range(NO // 512):
                widen(w5("GK", o0 + 512 * i), ind(kwin, w5(ob, c * CW + 32 * i, 32)), "A")
        parts = [("GA", db(2 ** 26)), ("GP", db(4096)), ("GK", db(1))] if kwin else [("GG", df(2 ** 50)), ("GP", db(2 ** 36))]
        for i in range(NO // 512):
            bk = kbank(c, i)
            for n, (nm, k) in enumerate(parts):
                mm([(w5(bk, 128 * j, 128), [(v(nm, o0 + 512 * i + j, o0 + 512 * i + 512, 4), k)]) for j in range(4)],
                   n == 0, n == len(parts) - 1, [(bk, 0, 512)])
            scan(w5("SC", o0 + 512 * i), v("DL"), v(bk), ALU.add, ALU.max)
        win = v("SC", o0 + 15, o0 + NO, 16)
        ts(w5("QI", 72 * c, 64), win, 4095 if kwin else 127, None, ALU.bitwise_and)
        lin("Q", w5("QB", c * QW + 16, 128), ind(w5("QI", 72 * c, 72), v("OQ")), 1.0, -2048.0)
        if not kwin:
            ts(w5("QI", 72 * (c + 2), 64), win, 8, 15, ALU.logical_shift_right, ALU.bitwise_and)
            lin("-", w5("QB", (c + 2) * QW + 16, 128), ind(w5("QI", 72 * (c + 2), 72), v("OQ")), -1.0, 2048.0)

    def gate(c, k, out, flag, x, op=ALU.mult):
        if op == ALU.mult:
            by = [lambda: mm([(sm(c, k), [(db(8192), flag), (df(1) if x[3] == F32 else db(1), x)])]),
                  lambda: act(out, sm(c, k), -8192.0, 1.0, AF.Relu)]
        else:
            by = [lambda: mm([(sm(c, k), [(df(1), flag), (df(1), x)])]), lambda: act(out, sm(c, k))]
        pick(P["gate"], {"A": by, "V": [None, lambda: tt(out, flag, x, op)]})

    def turn(c, e):
        return [(w5("QB", c * QW + 16 - 4 * k, 128), w5(e, k * CW, CW)) for k in range(2)]

    def goes(rd):
        for c in range(NC):
            x = L("PS7", c, 128)
            mm(([(x, [(db(8), L("BO", c))])] if rd == 2 else []) + swap(x, [(1, L("CP", c)), (-4, L("UP", c))]), True, True)
        for k in range(4):
            ts(w5("MK", 128 * k, 128), w5("PS7", 128, 128), float(k - 480), None, ALU.is_equal)
        scan(v("IK"), v("RS"), v("MK"), ALU.mult, ALU.add)
        mm([(v("PS6"), [(v("BLK"), v("IK")), (v("UT"), v("MK"))])])
        act(v("SG"), v("PS6"), CAP + 0.5 - 4096, -1.0, AF.Sign)
        mm([(w5("PS7", 128, 128), [(db(1), w5("SG", 128 * k, 128)) for k in range(4)])])
        lin("x", v("GS"), w5("PS7", 128, 128), 1.0, 0.0)

    CD = 32768 - 2048 + 15 + 3 * 2048
    cur[0] = -1
    for c in range(NC):
        mm(swap(sm(c, 7), [(1, L("BS", c))]))
        lin("x", L("BY", c), sm(c, 7), 1.0, 0.0)
    for rd in range(RO):
        for c in range(NC):
            cur[0] = c
            if rd == 0:
                draw(c, v("WT", 0, B), v("KD", 0, B), w5("N2", own, H), "OB", "OH")
            else:
                w = WT1 if rd == 1 else WTW
                draw(c, v("WT", 0, w), v("KD", 0, w), v("N1"), "OB", "OH")
            x = L("PS7", c)
            mm([(sm(c, 0), turn(c, "EE"))])
            mm([(x, [(db(1), L("BY", c))])] + (swap(x, [(611, L("TT", c, 128 * (rd - 1)))]) if rd else []) + [(x, turn(c, "E5"))], True, True)
            lin("o", L("OB2", c), sm(c, 0), 1.0, 2048.0)
            lin("h", L("H2", c), x, 1.0, 2.0 ** 21 + 1023.5)
            ts(L("H3", c), L("H2", c), H - 1, None, ALU.bitwise_and)
            lin("p", L("CP", c), sm(c, 0), 1 / 256, 167.5 + 1 / 512)
            lin("u", L("UP", c), sm(c, 0), 1 / 1024, 161.5 + 1 / 2048)
            mm([(sm(c, 2), [(db(1), v("CC", 0, 64)), (db(HX), v("CC", 64, 128)), (db(-37), L("CP", c)), (db(HX), L("CP", c)),
                            (db(-4 * HX), L("UP", c))])])
            tt(L("OH2", c), L("H3", c), sm(c, 2), ALU.add)
        if rd == 0:
            second()
        cur[0] = 1
        goes(rd)
        for c in range(NC):
            cur[0] = c
            o0 = c * NO
            draw(c, v("G2"), None, v("N2"), "OB2", "OH2")
            mm([(sm(c, 4), [(db(-2048 * k), L("MK", c, 128 * k)) for k in (1, 2, 3)] + turn(c, "E6") + turn(c + 2, "EE"))])
            lin("d", L("OR", c), sm(c, 4), 1.0, CD)
            lin("x", L("DV", c), sm(c, 4), 1.0, CD + 1)
            for i in range(NO // 512):
                a = o0 + 512 * i
                gi = ind(v("R2"), w5("OR", c * CW + 32 * i, 32))
                bk = v(kbank(c, i))
                by = [lambda: act(w5("GK", a), gi), lambda: mm([(bk, [(db(1), w5("ND0", a)), (db(-1), w5("GK", a))])])]
                pick(P["room"][(rd * NC + c) * 2 + i], {"A": by + [lambda: act(w5("VI", a), bk, 0.0, 1.0, AF.Relu)],
                                                        "V": [None, None, lambda: tt(w5("VI", a), gi, w5("ND0", a), ALU.is_lt)]})
            terms = [(db(-1), L("GS", c))]
            if rd:
                tt(L("EQ", c), L("DV", c), L("KV", c) if rd == 1 else L("S12", c), ALU.is_equal)
                terms.append((db(1), L("EQ", c)))
            if rd == 2:
                gate(c, 6, L("DA", c), L("NN", c), L("DV", c))
                gate(c, 7, L("DBB", c), L("NM", c), L("DV", c))
            terms += [(w5("SEL", 15 - r, 128), v("VI", o0 + r, o0 + NO, 16)) for r in range(16)]
            mm([(sm(c, 5), terms)])
            kp = L("KP", c, 128 * rd)
            pick("A", {"A": lambda: act(kp, sm(c, 5), 3.0, -1.0, AF.Relu), "V": lambda: ts(kp, sm(c, 5), 2.5, None, ALU.is_le)})
            if rd < 2:
                up = ([L("TT", c)] if rd else []) + [L("GS", c)]
                mm([(sm(c, 6), [(db(1), L("BB", c))] + [(dh(1237), x) for x in up] + [(dh(-1237), kp)]),
                    (sm(c, 7), [(db(1), L("BA", c))] + [(dh(-724), x) for x in up] + [(dh(724), kp)])])
                lin("b", L("OB", c), sm(c, 6), 1.0, 2048.0 + 4 * 1237)
                lin("n", L("OH", c), sm(c, 7), 1.0, 1024.0 - 4 * 724 + 3072)
                mm([(sm(c, 1), [(db(1), x) for x in up] + [(db(-1), kp)])])
                lin("x", L("TT", c, 128 * rd), sm(c, 1), 1.0, 4.0)
                gate(c, 3, L("KV", c, 128 * rd), kp, L("DV", c))
            if rd == 1:
                gate(c, 3, L("BO", c), L("KP", c), kp)
                gate(c, 3, L("S12", c), L("KV", c), L("KV", c, 128), ALU.add)
                gate(c, 3, L("U1", c), L("KP", c), L("KV", c, 128))
                tt(L("U2", c), L("S12", c), L("U1", c), ALU.subtract)
                act(L("B12", c), L("U1", c), -1.0)
                act(L("A12", c), L("U2", c), -1.0)
                act(L("NN", c), L("S12", c), 1.0, -1.0, AF.Relu)
                lin("x", L("NM", c), L("NN", c), -1.0, 1.0)
            if rd == 2:
                for y, dst, dv, old, tmp in (("YA", T.ya, "DA", "A12", "U1"), ("YB", T.yb, "DBB", "B12", "U2")):
                    gate(c, 1 + (y == "YA"), L(tmp, c), kp, L(dv, c))
                    tt(L(y, c), L(tmp, c), L(old, c), ALU.add)
                    dma(dst[:, c * CW:(c + 1) * CW], L(y, c)[0], 128 * CW * 4, L(y, c)[1], [])
    return ops, nsent


def schedule(ops):
    al = "0123456789abcdefghijklmnopqrstuvwxyzABCDEFGHIJKLMNOPQRSTUVWXYZ"
    order = [al.index(ORDER[k]) * 62 + al.index(ORDER[k + 1]) for k in range(0, len(ORDER), 2)]
    assert sorted(order) == list(range(len(ops)))
    last, done = {}, set()
    for i in order:
        o = ops[i]
        assert o["deps"] <= done
        done.add(i)
        for b in o["banks"]:
            o["deps"] |= set(j for q, j in last.get(b, {}).items() if q != o["q"])
            last.setdefault(b, {})[o["q"]] = i
        for d in list(o["deps"]):
            if ops[d]["kind"] == "n":
                o["deps"] = (o["deps"] - {d}) | ops[d]["deps"]
    return order


def rank_program(g, core, T, topo):
    rank = T.rank_of(core)
    if rank is None:
        return
    ops, nsent = build(g, T, topo, rank)
    order = schedule(ops)
    eng = {"V": g.vector, "A": g.scalar, "P": g.tensor, "G": g, "S": g.sync}
    cnt = {"V": 0, "A": 0, "P": 0, "G": 0}
    seen = {}
    for i in order:
        o = ops[i]
        if o["kind"] in "xn":
            continue
        need = {}
        for d in o["deps"]:
            p = ops[d]
            if p["q"] == o["q"] == "P":
                continue
            if p["kind"] == "c":
                key = "c" + p["q"]
                need[key] = (T.sem[key], max(p["n"], need.get(key, (0, 0))[1]))
            else:
                need["op%d" % d] = p["sem"]
        for key, (sem, val) in need.items():
            if seen.get((o["q"], key), 0) < val:
                eng[o["q"]].wait_ge(sem, val)
                seen[(o["q"], key)] = val
        ins = o["fn"]()
        if o["kind"] == "c":
            cnt[o["q"]] += 1
            o["n"] = cnt[o["q"]]
            ins.then_inc(T.sem["c" + o["q"]], 1)
        elif o["kind"] == "d":
            ins.then_inc(o["sem"][0], 16)
    for q in cnt:
        g.wait_ge(T.sem["c" + q], cnt[q])
    g.wait_ge(T.sem.sent, nsent)
    for o in ops:
        if o["kind"] in "dx":
            g.wait_ge(o["sem"][0], o["sem"][1])
